import numpy as np
import ml_dtypes


def mxq(x, axis, fmt="e4m3"):
    dtype, down = {"e4m3": (ml_dtypes.float8_e4m3fn, 7), "e5m2": (ml_dtypes.float8_e5m2, 14)}[fmt]
    v = np.moveaxis(np.asarray(x, np.float32).astype(ml_dtypes.bfloat16).astype(np.float64), axis, -1)
    blocks = v.reshape(v.shape[:-1] + (-1, 32))
    amax = np.abs(blocks).max(-1, keepdims=True)
    byte = np.maximum(np.where(amax > 0, np.frexp(amax)[1] - 1 + 127, 0) - down, 1)
    scale = np.exp2(byte - 127.0)
    codes = (blocks / scale).astype(np.float32).astype(dtype).astype(np.float64)
    return np.moveaxis((codes * scale).reshape(v.shape), -1, axis)


WIDE = False


def mx_kscale(k):
    if not WIDE:
        return np.ones(k)
    levels = np.array([10, -10, 5, -5, 0])
    if k % 512:
        return np.exp2(np.random.permutation(np.resize(levels, k // 32))).repeat(32)
    a = np.empty((k // 512, 16))
    for p in range(k // 512):
        a[p, :8] = np.random.permutation(np.resize(levels, 8))
        for g in range(8):
            far = levels[np.abs(levels - a[p, g]) >= 10]
            a[p, g + 8] = far[np.random.randint(len(far))]
    return np.exp2(a.ravel()).repeat(32)


BF16 = ml_dtypes.bfloat16


def bf(x):
    return np.asarray(x, np.float32).astype(BF16)


def f64(x):
    return np.asarray(x).astype(np.float64)


E2M1 = np.array([0.0, 0.5, 1.0, 1.5, 2.0, 3.0, 4.0, 6.0, -0.0, -0.5, -1.0, -1.5, -2.0, -3.0, -4.0, -6.0])


def pack_weight(w, fmt):
    k, n = w.shape
    w = f64(bf(w)).reshape(k // 32, 32, n)
    amax = np.abs(w).max(1)
    if fmt == "e4m3":
        byte = np.frexp(amax)[1] - 1 + 127 - 7
    else:
        mant, ex = np.frexp(amax / 6.0)
        byte = np.where(mant > 0.5, ex, ex - 1) + 127
    byte = np.clip(np.where(amax > 0, byte, 1), 1, 254)
    scaled = (w * np.exp2(127.0 - byte)[:, None, :]).reshape(k, n).astype(np.float32)
    by_word = np.ascontiguousarray(scaled.reshape(k // 512, 128, 4, n).transpose(0, 1, 3, 2))
    if fmt == "e4m3":
        words = by_word.astype(ml_dtypes.float8_e4m3fn).view(np.uint8)
    else:
        c = by_word.astype(ml_dtypes.float4_e2m1fn).view(np.uint8) & 0xF
        words = c[..., 0::2] | (c[..., 1::2] << 4)
    return np.ascontiguousarray(words), np.ascontiguousarray(byte.astype(np.uint8).reshape(k // 512, 16, n))


def unpack_weight(words, scales, fmt):
    g, p, n, _ = words.shape
    if fmt == "e4m3":
        vals = np.ascontiguousarray(words).view(ml_dtypes.float8_e4m3fn).astype(np.float64)
    else:
        nib = np.empty((g, p, n, 4), np.uint8)
        nib[..., 0::2] = words & 0xF
        nib[..., 1::2] = words >> 4
        vals = E2M1[nib]
    vals = vals * np.repeat(np.exp2(scales.astype(np.float64) - 127.0), 8, axis=1)[..., None]
    return vals.transpose(0, 1, 3, 2).reshape(g * 512, n)
def pack4(w):
    words, scales = pack_weight(w, "e2m1")
    return words.reshape(words.shape[0], 128, -1), scales


def unpack4(words, scales):
    return unpack_weight(words.reshape(words.shape[0], 128, -1, 2), scales, "e2m1")


I, B, G, C, F = 512, 1024, 2048, 512, 1024


def draw0():
    s = mx_kscale(B)
    u = mx_kscale(C)
    t = mx_kscale(G)
    initial = np.random.standard_normal((I, B)) * s
    raising = np.random.standard_normal((B, G)) / np.sqrt(B) / G ** 0.25
    lowering = np.random.standard_normal((G, C)) / np.sqrt(C) / G ** 0.25
    final = np.random.standard_normal((C, F)) / u[:, None]
    raising_words, raising_scales = pack4(raising / s[:, None] * t)
    return {"initial": bf(initial),
            "raising_words": raising_words,
            "raising_scales": raising_scales,
            "squeeze": bf(1 + 0.1 * np.random.standard_normal(G)),
            "lowering": bf(lowering * u / t[:, None]),
            "final": bf(final),
            "population": bf(np.random.uniform(0.25, 1.75, I))}


def core(initial, raising_words, raising_scales, squeeze, lowering, final, population):
    left = mxq(f64(initial), 1, "e4m3") @ unpack4(raising_words, raising_scales)
    left = left * f64(squeeze)
    right = mxq(f64(lowering), 1, "e4m3") @ mxq(f64(final), 0, "e4m3")
    overlap = mxq(left, 1, "e4m3") @ mxq(right, 0, "e4m3")
    strength = np.square(overlap) * f64(population)[:, None]
    return overlap, strength


def e4m3fn_bytes(y):
    return np.clip(np.asarray(y, np.float64), -448.0, 448.0).astype(np.float32).astype(ml_dtypes.float8_e4m3fn).view(np.uint8)


def e4m3fn_values(b):
    return np.asarray(b, np.uint8).view(ml_dtypes.float8_e4m3fn).astype(np.float64)


def setup_inputs():
    d = draw0()
    x0 = np.asarray(d['initial']).astype(np.float64)
    s = (np.max(np.abs(x0), axis=(0,), keepdims=True) / 448.0).astype(np.float32)
    out = {}
    for k, v in d.items():
        if k == 'initial':
            out['initial_bytes'] = e4m3fn_bytes(x0 / s.astype(np.float64))
            out['initial_scale'] = s
        else:
            out[k] = v
    return out


def reference(initial_bytes, initial_scale, raising_words, raising_scales, squeeze, lowering, final, population):
    return core(e4m3fn_values(initial_bytes) * initial_scale.astype(np.float64), raising_words, raising_scales, squeeze, lowering, final, population)

@@ -1,0 +1,484 @@
+from contextlib import ExitStack
+
+import concourse.mybir as mybir
+from concourse.masks import make_identity
+
+I, B, G, C, F = 512, 1024, 2048, 512, 1024
+FLOPS = 2 * I * B * G + 2 * G * C * F + 2 * I * G * F
+
+F32 = mybir.dt.float32
+BF16 = mybir.dt.bfloat16
+I32 = mybir.dt.int32
+U32 = mybir.dt.uint32
+U8 = mybir.dt.uint8
+FP8 = mybir.dt.float8_e4m3fn
+FP8X4 = mybir.dt.float8_e4m3fn_x4
+FP4X4 = mybir.dt.float4_e2m1fn_x4
+MULT = mybir.AluOpType.mult
+
+P = 128
+NA = I // P
+NG = G // 512
+NQ = 4
+FQ = F // NQ
+
+
+def tile_franck_condon_overlap_table_s11_kernel(
+    tc, initial_bytes, initial_scale, raising_words, raising_scales, squeeze, lowering, final, population, out_0, out_1
+):
+    nc = tc.nc
+    with ExitStack() as ctx:
+        sb = ctx.enter_context(tc.tile_pool(name="sb", bufs=1))
+        ps = ctx.enter_context(tc.psum_pool(name="ps", bufs=8))
+
+        def keep(name, shape, dtype):
+            t = sb.tile(shape, dtype, name=name, tag=name, align_bytes=256)
+            return t
+
+        def bank(name, dtype=F32):
+            t = ps.tile([P, 512], dtype, name=name, tag="bank")
+            return t
+
+        scale_bc = keep("scale_bc", [P, B], F32)
+        ibytes = keep("ibytes", [P, NA, B], U8)
+        low_raw = [keep("low_raw%d" % g, [P, 4, C], BF16) for g in range(NG)]
+        fin_raw = [keep("fin_raw%d" % h, [P, 4, 512], BF16) for h in range(2)]
+        w_raw = [keep("w_raw%d" % g, [P, 2 * G], U8) for g in range(2)]
+        ws_raw = keep("ws_raw", [P, 2, G], U8)
+        sq_rows = keep("sq_rows", [P, P], BF16)
+        pop = keep("pop", [P, NA], BF16)
+
+        ident = keep("ident", [P, P], F32)
+        identb = keep("identb", [P, P], BF16)
+        perm = keep("perm", [P, P], F32)
+        warm = keep("warm", [P, 1], F32)
+        ctx.enter_context(tc.manual_schedule())
+        low_v = lowering.rearrange("(g p t) c -> g p t c", p=P, t=4)
+        ib_v = initial_bytes.rearrange("(p a) k -> p a k", a=NA)
+        fin_v = final.rearrange("(p j) f -> p j f", j=4)
+        nc.vector.memset(ws_raw[:].rearrange("p g n -> p (g n)").bitcast(I32), 0)
+        nc.vector.memset(sq_rows[:], 0.0)
+        nc.vector.memset(warm[:], 0.0)
+        nc.scalar.copy(out=warm[:], in_=warm[:])
+        make_identity(nc, ident[:])
+        make_identity(nc, identb[:])
+        nc.sync.dma_start(out=low_raw[0][:], in_=low_v[0])
+        nc.sync.dma_start(out=fin_raw[0][:], in_=fin_v[:, :, 0:512])
+        nc.sync.dma_start(out=scale_bc[:], in_=initial_scale.rearrange("o k -> (o k)").partition_broadcast(P))
+        nc.sync.dma_start(out=ibytes[:, 0:2, :], in_=ib_v[:, 0:2, :])
+        nc.sync.dma_start(out=low_raw[1][:], in_=low_v[1])
+        nc.sync.dma_start(out=w_raw[0][:].bitcast(I32), in_=raising_words[0].bitcast(I32))
+        nc.sync.dma_start(out=w_raw[1][:].bitcast(I32), in_=raising_words[1].bitcast(I32))
+        for q in range(4):
+            nc.sync.dma_start(
+                out=ws_raw[32 * q : 32 * q + 4, :, :].bitcast(I32),
+                in_=raising_scales[:, 4 * q : 4 * q + 4, :].rearrange("g q n -> q g n").bitcast(I32),
+            )
+        nc.sync.dma_start(out=ibytes[:, 2:4, :], in_=ib_v[:, 2:4, :])
+        nc.sync.dma_start(out=low_raw[2][:], in_=low_v[2])
+        nc.sync.dma_start(out=low_raw[3][:], in_=low_v[3])
+        nc.sync.dma_start(out=fin_raw[1][:], in_=fin_v[:, :, 512:1024])
+        for g in range(NG):
+            nc.scalar.dma_start(
+                out=sq_rows[4 * g : 4 * g + 4, :].rearrange("t (q r) -> t q r", r=8),
+                in_=squeeze[512 * g : 512 * g + 512].rearrange("(q t r) -> t q r", q=16, t=4),
+            )
+        nc.scalar.dma_start(out=pop[:], in_=population.rearrange("(p a) -> p a", a=NA))
+        nc.vector.tensor_copy(
+            out=perm[:].rearrange("p (t q h) -> p t q h", t=4, q=16), in_=ident[:].rearrange("p (q t h) -> p t q h", q=16, t=4)
+        )
+
+        LOWE, IE, FC, WSPLIT = "SSSSSSSS", "SSSS", "SSVS", 1
+        E2V = [(1, 1, 0),(1, 1, 1),(3, 0, 1),(3, 3, 0)]
+
+        low_grp = [keep("low_grp%d" % g, [P, 2048], BF16) for g in range(NG)]
+        low_q = [keep("low_q%d" % g, [P, 512], U32) for g in range(NG)]
+        low_s = [keep("low_s%d" % g, [P, 512], U8) for g in range(NG)]
+        ini = keep("ini", [P, NA, B], BF16)
+        ini_grp = [keep("ini_grp%d" % a, [P, 1024], BF16) for a in range(NA)]
+        ini_q = [keep("ini_q%d" % a, [P, 256], U32) for a in range(NA)]
+        ini_s = [keep("ini_s%d" % a, [P, 256], U8) for a in range(NA)]
+        fin_grp = [keep("fin_grp%d" % f, [P, 1024], BF16) for f in range(NQ)]
+        fin_q = [keep("fin_q%d" % f, [P, FQ], U32) for f in range(NQ)]
+        fin_s = [keep("fin_s%d" % f, [P, FQ], U8) for f in range(NQ)]
+        w_q = [keep("w_q%d" % g, [P, 2 * G], U8) for g in range(2)]
+        w_s = keep("w_s", [P, 2, G], U8)
+        sq = keep("sq", [P, 16], F32)
+        left_grp = [keep("left_grp%d" % a, [P, NG * 512], BF16) for a in range(NA)]
+        left_q = [keep("left_q%d" % a, [P, NG * P], U32) for a in range(NA)]
+        left_s = [keep("left_s%d" % a, [P, NG * P], U8) for a in range(NA)]
+        right_grp = {}
+        right_q = [keep("right_q%d" % f, [P, NG * FQ], U32) for f in range(NQ)]
+        right_s = [keep("right_s%d" % f, [P, NG * FQ], U8) for f in range(NQ)]
+        ov = keep("ov", [P, NA, F], F32)
+        st = keep("st", [P, NA, F], F32)
+        out0_v = out_0.rearrange("(p a) f -> p a f", a=NA)
+        out1_v = out_1.rearrange("(p a) f -> p a f", a=NA)
+        banks = {}
+
+        def copy(eng, out, in_):
+            if eng == "S":
+                nc.scalar.copy(out=out, in_=in_)
+            else:
+                nc.vector.tensor_copy(out=out, in_=in_)
+
+        def lowT(g, h):
+            words = low_raw[g][:].rearrange("p t c -> p (t c)").bitcast(F32)
+            xt = bank("xt")
+            banks[("x", g, h)] = xt
+            for x in range(4):
+                rl, u = 2 * h + x // 2, x % 2
+                nc.tensor.transpose(xt[:, x * P : (x + 1) * P], words[:, 256 * rl + u : 256 * (rl + 1) : 2], perm[:])
+
+        def lowE(g, h):
+            dst = low_grp[g][:].bitcast(F32).rearrange("p (j x) -> p j x", x=8)
+            copy(LOWE[2 * g + h], dst[:, :, 4 * h : 4 * h + 4], banks[("x", g, h)][:].rearrange("p (x j) -> p j x", x=4))
+
+        def lowQ(g):
+            nc.vector.quantize_mx(out=low_q[g][:].bitcast(FP8X4), scales=low_s[g][:], in_=low_grp[g][:])
+
+        def iM(a):
+            nc.vector.tensor_tensor(out=ini[:, a, :], in0=ibytes[:, a, :].bitcast(FP8), in1=scale_bc[:], op=MULT)
+
+        def iT(a):
+            words = ini[:, a, :].bitcast(F32)
+            xt = bank("xt")
+            banks[("y", a)] = xt
+            for g in range(2):
+                for u in range(2):
+                    x = 2 * g + u
+                    nc.tensor.transpose(xt[:, x * P : (x + 1) * P], words[:, 256 * g + u : 256 * (g + 1) : 2], ident[:])
+
+        def iE(a):
+            copy(
+                IE[a],
+                ini_grp[a][:].bitcast(F32).rearrange("p (g m u) -> p g m u", g=2, u=2),
+                banks[("y", a)][:].rearrange("p (g u m) -> p g m u", g=2, u=2),
+            )
+
+        def iQ(a):
+            nc.vector.quantize_mx(out=ini_q[a][:].bitcast(FP8X4), scales=ini_s[a][:], in_=ini_grp[a][:])
+
+        def fC(f):
+            cols = slice((f % 2) * FQ, (f % 2) * FQ + FQ)
+            copy(FC[f], fin_grp[f][:].rearrange("p (f j) -> p f j", j=4), fin_raw[f // 2][:, :, cols].rearrange("p j f -> p f j"))
+
+        def fQ(f):
+            nc.vector.quantize_mx(out=fin_q[f][:].bitcast(FP8X4), scales=fin_s[f][:], in_=fin_grp[f][:])
+
+        def wP(g):
+            for h in range(WSPLIT):
+                n = 4096 // WSPLIT
+                cols = slice(n * h, n * (h + 1))
+                nc.vector.tensor_copy(
+                    out=w_q[g][:, cols].bitcast(I32).rearrange("p (b t q w) -> p b t q w", t=4, q=16, w=4),
+                    in_=w_raw[g][:, cols].bitcast(I32).rearrange("p (b q t w) -> p b t q w", t=4, q=16, w=4),
+                )
+
+        def sP():
+            for g in range(2):
+                nc.vector.tensor_copy(
+                    out=w_s[:, g, :].bitcast(I32).rearrange("p (b t q w) -> p b t q w", t=4, q=16, w=2),
+                    in_=ws_raw[:, g, :].bitcast(I32).rearrange("p (b q t w) -> p b t q w", t=4, q=16, w=2),
+                )
+
+        def sqT():
+            banks["sq"] = bank("sqt", BF16)
+            nc.tensor.transpose(banks["sq"][:, 0:P], sq_rows[:], identb[:])
+
+        def sqE():
+            nc.vector.tensor_copy(out=sq[:], in_=banks["sq"][:, 0:16])
+
+        def S1(a, gg):
+            acc = bank("acc")
+            banks[("l", a, gg)] = acc
+            for t in range(4):
+                j = 4 * gg + t
+                for g in range(2):
+                    nc.tensor.matmul_mx(
+                        out=acc[:, t * P : (t + 1) * P],
+                        lhsT=w_q[g][:, 256 * j : 256 * (j + 1)].bitcast(FP4X4),
+                        lhsT_scale=w_s[:, g, P * j : P * (j + 1)],
+                        rhs=ini_q[a][:, g * P : (g + 1) * P].bitcast(FP8X4),
+                        rhs_scale=ini_s[a][:, g * P : (g + 1) * P],
+                        start=(g == 0),
+                        stop=(g == 1),
+                    )
+
+        def E1(a, gg):
+            nc.vector.tensor_tensor(
+                out=left_grp[a][:, 512 * gg : 512 * (gg + 1)].rearrange("p (m t) -> p m t", t=4),
+                in0=banks[("l", a, gg)][:].rearrange("p (t m) -> p m t", t=4),
+                in1=sq[:, 4 * gg : 4 * gg + 4].unsqueeze(1).to_broadcast([P, P, 4]),
+                op=MULT,
+            )
+
+        def Q1(a, h):
+            nc.vector.quantize_mx(
+                out=left_q[a][:, 256 * h : 256 * (h + 1)].bitcast(FP8X4),
+                scales=left_s[a][:, 256 * h : 256 * (h + 1)],
+                in_=left_grp[a][:, 1024 * h : 1024 * (h + 1)],
+            )
+
+        def S2(f, gg, c):
+            acc = bank("acc")
+            banks[("r", f, gg, c)] = acc
+            for t in range(4):
+                nc.tensor.matmul_mx(
+                    out=acc[:, t * P : (t + 1) * P],
+                    lhsT=low_q[gg][:, t * P : (t + 1) * P].bitcast(FP8X4),
+                    lhsT_scale=low_s[gg][:, t * P : (t + 1) * P],
+                    rhs=fin_q[f][:, c * P : (c + 1) * P].bitcast(FP8X4),
+                    rhs_scale=fin_s[f][:, c * P : (c + 1) * P],
+                    start=True,
+                    stop=True,
+                )
+
+        def E2(f, gg, c):
+            if f not in right_grp:
+                right_grp[f] = sb.tile([P, NG * 4 * FQ], BF16, name="right_grp%d" % f, tag="right_grp", bufs=2, align_bytes=256)
+            dst = right_grp[f][:, 1024 * gg + 512 * c : 1024 * gg + 512 * (c + 1)].rearrange("p (f t) -> p f t", t=4)
+            copy("V" if (f, gg, c) in E2V else "S", dst, banks[("r", f, gg, c)][:].rearrange("p (t f) -> p f t", t=4))
+
+        def Q2(f, h):
+            nc.vector.quantize_mx(
+                out=right_q[f][:, 512 * h : 512 * (h + 1)].bitcast(FP8X4),
+                scales=right_s[f][:, 512 * h : 512 * (h + 1)],
+                in_=right_grp[f][:, 2048 * h : 2048 * (h + 1)],
+            )
+
+        def S3(a, f):
+            acc = bank("acc")
+            banks[("o", a, f)] = acc
+            for gg in range(NG):
+                nc.tensor.matmul_mx(
+                    out=acc[:, 0:FQ],
+                    lhsT=left_q[a][:, gg * P : (gg + 1) * P].bitcast(FP8X4),
+                    lhsT_scale=left_s[a][:, gg * P : (gg + 1) * P],
+                    rhs=right_q[f][:, gg * FQ : (gg + 1) * FQ].bitcast(FP8X4),
+                    rhs_scale=right_s[f][:, gg * FQ : (gg + 1) * FQ],
+                    start=(gg == 0),
+                    stop=(gg == NG - 1),
+                )
+
+        def OV(a, f):
+            cols = slice(f * FQ, (f + 1) * FQ)
+            nc.scalar.copy(out=ov[:, a, cols], in_=banks[("o", a, f)][:, 0:FQ])
+            nc.sync.dma_start(out=out0_v[:, a, cols], in_=ov[:, a, cols])
+
+        def ST(a, f):
+            cols = slice(f * FQ, (f + 1) * FQ)
+            nc.vector.scalar_tensor_tensor(
+                out=st[:, a, cols], in0=banks[("o", a, f)][:, 0:FQ], scalar=pop[:, a : a + 1], in1=ov[:, a, cols], op0=MULT, op1=MULT
+            )
+            nc.sync.dma_start(out=out1_v[:, a, cols], in_=st[:, a, cols])
+
+        lowT(0, 0)
+        lowT(0, 1)
+        lowE(0, 0)
+        lowE(0, 1)
+        fC(0)
+        lowQ(0)
+        iM(0)
+        fC(1)
+        fQ(0)
+        lowT(1, 1)
+        iM(1)
+        iT(0)
+        lowE(1, 1)
+        lowT(1, 0)
+        iE(0)
+        wP(0)
+        iT(1)
+        lowE(1, 0)
+        iQ(0)
+        S2(0, 0, 1)
+        fQ(1)
+        iE(1)
+        S2(0, 0, 0)
+        lowQ(1)
+        S2(1, 0, 0)
+        E2(0, 0, 1)
+        S2(1, 0, 1)
+        wP(1)
+        E2(0, 0, 0)
+        S2(0, 1, 0)
+        S2(0, 1, 1)
+        iQ(1)
+        E2(0, 1, 0)
+        S2(1, 1, 1)
+        iM(2)
+        lowT(2, 1)
+        E2(0, 1, 1)
+        lowT(2, 0)
+        E2(1, 0, 1)
+        Q2(0, 0)
+        iT(2)
+        lowE(2, 1)
+        iM(3)
+        lowT(3, 0)
+        lowE(2, 0)
+        lowT(3, 1)
+        iE(2)
+        sqT()
+        sP()
+        iT(3)
+        lowE(3, 0)
+        S2(1, 1, 0)
+        lowQ(2)
+        lowE(3, 1)
+        S1(1, 0)
+        iE(3)
+        iQ(2)
+        fC(2)
+        S2(0, 2, 1)
+        E2(1, 0, 0)
+        S1(0, 0)
+        iQ(3)
+        E2(0, 2, 1)
+        lowQ(3)
+        sqE()
+        S1(0, 2)
+        fC(3)
+        E1(0, 0)
+        S1(0, 1)
+        E1(0, 2)
+        S2(0, 3, 0)
+        S2(0, 3, 1)
+        E1(0, 1)
+        E2(0, 3, 0)
+        S1(0, 3)
+        fQ(2)
+        E2(0, 3, 1)
+        Q1(0, 0)
+        S2(0, 2, 0)
+        S2(2, 1, 1)
+        E1(0, 3)
+        E2(0, 2, 0)
+        S2(1, 2, 0)
+        E1(1, 0)
+        S1(1, 1)
+        E2(2, 1, 1)
+        Q1(0, 1)
+        E2(1, 2, 0)
+        S1(1, 2)
+        E2(1, 1, 0)
+        S2(1, 3, 0)
+        E2(1, 1, 1)
+        S1(2, 2)
+        E2(1, 3, 0)
+        Q2(0, 1)
+        S2(2, 0, 1)
+        Q2(1, 0)
+        S2(1, 3, 1)
+        E2(2, 0, 1)
+        S1(1, 3)
+        E1(2, 2)
+        E2(1, 3, 1)
+        S2(2, 0, 0)
+        E1(1, 2)
+        S1(2, 0)
+        E2(2, 0, 0)
+        E1(1, 3)
+        S3(0, 0)
+        E1(1, 1)
+        S1(2, 1)
+        OV(0, 0)
+        Q1(1, 1)
+        Q1(1, 0)
+        S2(2, 2, 0)
+        E1(2, 0)
+        S2(2, 1, 0)
+        E2(2, 2, 0)
+        S3(1, 0)
+        E1(2, 1)
+        E2(2, 1, 0)
+        S2(2, 2, 1)
+        ST(0, 0)
+        S2(2, 3, 1)
+        OV(1, 0)
+        Q2(2, 0)
+        S2(2, 3, 0)
+        E2(2, 2, 1)
+        S1(3, 0)
+        ST(1, 0)
+        E2(2, 3, 0)
+        Q1(2, 0)
+        S2(1, 2, 1)
+        E2(2, 3, 1)
+        E1(3, 0)
+        S1(3, 1)
+        E2(1, 2, 1)
+        fQ(3)
+        S1(2, 3)
+        Q2(2, 1)
+        S2(3, 3, 0)
+        Q2(1, 1)
+        S2(3, 0, 1)
+        S2(3, 0, 0)
+        E1(2, 3)
+        S3(1, 1)
+        E2(3, 0, 0)
+        E2(3, 0, 1)
+        S3(0, 1)
+        OV(1, 1)
+        Q1(2, 1)
+        S2(3, 1, 0)
+        E2(3, 3, 0)
+        OV(0, 1)
+        S3(2, 1)
+        E2(3, 1, 0)
+        ST(0, 1)
+        S2(3, 1, 1)
+        ST(1, 1)
+        OV(2, 1)
+        S2(3, 2, 0)
+        E1(3, 1)
+        E2(3, 1, 1)
+        S3(0, 2)
+        ST(2, 1)
+        E2(3, 2, 0)
+        S2(3, 2, 1)
+        Q1(3, 0)
+        S3(2, 0)
+        OV(0, 2)
+        Q2(3, 0)
+        E2(3, 2, 1)
+        S1(3, 2)
+        ST(0, 2)
+        OV(2, 0)
+        S2(3, 3, 1)
+        E1(3, 2)
+        S3(1, 2)
+        E2(3, 3, 1)
+        ST(2, 0)
+        S1(3, 3)
+        OV(1, 2)
+        Q2(3, 1)
+        S3(2, 2)
+        ST(1, 2)
+        S3(0, 3)
+        E1(3, 3)
+        OV(2, 2)
+        S3(1, 3)
+        ST(2, 2)
+        OV(0, 3)
+        Q1(3, 1)
+        S3(2, 3)
+        ST(0, 3)
+        OV(1, 3)
+        S3(3, 1)
+        ST(1, 3)
+        OV(2, 3)
+        S3(3, 0)
+        ST(2, 3)
+        OV(3, 1)
+        S3(3, 3)
+        ST(3, 1)
+        OV(3, 0)
+        S3(3, 2)
+        ST(3, 0)
+        OV(3, 3)
+        ST(3, 3)
+        OV(3, 2)
+        ST(3, 2)

@@ -39,7 +39,7 @@ def tile_franck_condon_overlap_table_s11_kernel(
             t = ps.tile([P, 512], dtype, name=name, tag="bank")
             return t
 
-        scale_bc = keep("scale_bc", [P, B], F32)
+        sc = keep("sc", [P, 2, 4], F32)
         ibytes = keep("ibytes", [P, NA, B], U8)
         low_raw = [keep("low_raw%d" % g, [P, 4, C], BF16) for g in range(NG)]
         fin_raw = [keep("fin_raw%d" % h, [P, 4, 512], BF16) for h in range(2)]
@@ -47,7 +47,6 @@ def tile_franck_condon_overlap_table_s11_kernel(
         ws_raw = keep("ws_raw", [P, 2, G], U8)
         sq_rows = keep("sq_rows", [P, P], BF16)
         pop = keep("pop", [P, NA], BF16)
-
         ident = keep("ident", [P, P], F32)
         identb = keep("identb", [P, P], BF16)
         perm = keep("perm", [P, P], F32)
@@ -59,24 +58,25 @@ def tile_franck_condon_overlap_table_s11_kernel(
         nc.vector.memset(ws_raw[:].rearrange("p g n -> p (g n)").bitcast(I32), 0)
         nc.vector.memset(sq_rows[:], 0.0)
         nc.vector.memset(warm[:], 0.0)
+        nc.scalar.dma_start(out=sc[:], in_=initial_scale.rearrange("o (g p t) -> p (o g) t", p=P, t=4))
         nc.scalar.copy(out=warm[:], in_=warm[:])
         make_identity(nc, ident[:])
         make_identity(nc, identb[:])
-        nc.sync.dma_start(out=low_raw[0][:], in_=low_v[0])
-        nc.sync.dma_start(out=fin_raw[0][:], in_=fin_v[:, :, 0:512])
-        nc.sync.dma_start(out=scale_bc[:], in_=initial_scale.rearrange("o k -> (o k)").partition_broadcast(P))
         nc.sync.dma_start(out=ibytes[:, 0:2, :], in_=ib_v[:, 0:2, :])
+        nc.sync.dma_start(out=low_raw[0][:, 0:2, :], in_=low_v[0][:, 0:2, :])
+        nc.sync.dma_start(out=fin_raw[0][:], in_=fin_v[:, :, 0:512])
+        nc.sync.dma_start(out=low_raw[0][:, 2:4, :], in_=low_v[0][:, 2:4, :])
         nc.sync.dma_start(out=low_raw[1][:], in_=low_v[1])
-        nc.sync.dma_start(out=w_raw[0][:].bitcast(I32), in_=raising_words[0].bitcast(I32))
-        nc.sync.dma_start(out=w_raw[1][:].bitcast(I32), in_=raising_words[1].bitcast(I32))
+        nc.sync.dma_start(out=ibytes[:, 2:4, :], in_=ib_v[:, 2:4, :])
+        nc.sync.dma_start(out=low_raw[2][:], in_=low_v[2])
         for q in range(4):
             nc.sync.dma_start(
                 out=ws_raw[32 * q : 32 * q + 4, :, :].bitcast(I32),
                 in_=raising_scales[:, 4 * q : 4 * q + 4, :].rearrange("g q n -> q g n").bitcast(I32),
             )
-        nc.sync.dma_start(out=ibytes[:, 2:4, :], in_=ib_v[:, 2:4, :])
-        nc.sync.dma_start(out=low_raw[2][:], in_=low_v[2])
         nc.sync.dma_start(out=low_raw[3][:], in_=low_v[3])
+        nc.sync.dma_start(out=w_raw[0][:].bitcast(I32), in_=raising_words[0].bitcast(I32))
+        nc.sync.dma_start(out=w_raw[1][:].bitcast(I32), in_=raising_words[1].bitcast(I32))
         nc.sync.dma_start(out=fin_raw[1][:], in_=fin_v[:, :, 512:1024])
         for g in range(NG):
             nc.scalar.dma_start(
@@ -88,9 +88,8 @@ def tile_franck_condon_overlap_table_s11_kernel(
             out=perm[:].rearrange("p (t q h) -> p t q h", t=4, q=16), in_=ident[:].rearrange("p (q t h) -> p t q h", q=16, t=4)
         )
 
-        LOWE, IE, FC, WSPLIT = "SSSSSSSS", "SSSS", "SSVS", 1
-        E2V = [(1, 1, 0),(1, 1, 1),(3, 0, 1),(3, 3, 0)]
-
+        LOWE, IK, FC, WSPLIT = "SSSVSSSS", "VSSS", "SVSV", 1
+        E2V = [(3, 2, 1)]
         low_grp = [keep("low_grp%d" % g, [P, 2048], BF16) for g in range(NG)]
         low_q = [keep("low_q%d" % g, [P, 512], U32) for g in range(NG)]
         low_s = [keep("low_s%d" % g, [P, 512], U8) for g in range(NG)]
@@ -137,8 +136,12 @@ def tile_franck_condon_overlap_table_s11_kernel(
         def lowQ(g):
             nc.vector.quantize_mx(out=low_q[g][:].bitcast(FP8X4), scales=low_s[g][:], in_=low_grp[g][:])
 
-        def iM(a):
-            nc.vector.tensor_tensor(out=ini[:, a, :], in0=ibytes[:, a, :].bitcast(FP8), in1=scale_bc[:], op=MULT)
+        def iK(a):
+            src = ibytes[:, a, :].bitcast(FP8)
+            if IK[a] == "V":
+                nc.vector.tensor_copy(out=ini[:, a, :], in_=src)
+            else:
+                nc.scalar.copy(out=ini[:, a, :], in_=src)
 
         def iT(a):
             words = ini[:, a, :].bitcast(F32)
@@ -149,11 +152,13 @@ def tile_franck_condon_overlap_table_s11_kernel(
                     x = 2 * g + u
                     nc.tensor.transpose(xt[:, x * P : (x + 1) * P], words[:, 256 * g + u : 256 * (g + 1) : 2], ident[:])
 
-        def iE(a):
-            copy(
-                IE[a],
-                ini_grp[a][:].bitcast(F32).rearrange("p (g m u) -> p g m u", g=2, u=2),
-                banks[("y", a)][:].rearrange("p (g u m) -> p g m u", g=2, u=2),
+        def iE(a, g):
+            codes = banks[("y", a)][:, 256 * g : 256 * (g + 1)].bitcast(BF16)
+            nc.vector.tensor_tensor(
+                out=ini_grp[a][:, 512 * g : 512 * (g + 1)].rearrange("p (m u e) -> p m u e", u=2, e=2),
+                in0=codes.rearrange("p (u m e) -> p m u e", u=2, e=2),
+                in1=sc[:, g, :].rearrange("p (u e) -> p u e", u=2).unsqueeze(1).to_broadcast([P, P, 2, 2]),
+                op=MULT,
             )
 
         def iQ(a):
@@ -273,212 +278,216 @@ def tile_franck_condon_overlap_table_s11_kernel(
             )
             nc.sync.dma_start(out=out1_v[:, a, cols], in_=st[:, a, cols])
 
+        iK(1)
+        fC(0)
         lowT(0, 0)
+        iK(0)
+        iT(0)
         lowT(0, 1)
         lowE(0, 0)
-        lowE(0, 1)
-        fC(0)
-        lowQ(0)
-        iM(0)
-        fC(1)
-        fQ(0)
-        lowT(1, 1)
-        iM(1)
-        iT(0)
-        lowE(1, 1)
-        lowT(1, 0)
-        iE(0)
-        wP(0)
         iT(1)
-        lowE(1, 0)
-        iQ(0)
-        S2(0, 0, 1)
+        lowE(0, 1)
+        lowT(1, 1)
+        lowT(1, 0)
+        iE(0, 0)
+        iK(3)
+        fC(1)
         fQ(1)
-        iE(1)
-        S2(0, 0, 0)
-        lowQ(1)
-        S2(1, 0, 0)
-        E2(0, 0, 1)
-        S2(1, 0, 1)
-        wP(1)
-        E2(0, 0, 0)
-        S2(0, 1, 0)
-        S2(0, 1, 1)
-        iQ(1)
-        E2(0, 1, 0)
-        S2(1, 1, 1)
-        iM(2)
-        lowT(2, 1)
-        E2(0, 1, 1)
+        iE(1, 0)
+        fQ(0)
         lowT(2, 0)
-        E2(1, 0, 1)
-        Q2(0, 0)
-        iT(2)
-        lowE(2, 1)
-        iM(3)
+        iT(3)
+        iE(0, 1)
+        iK(2)
+        lowT(2, 1)
         lowT(3, 0)
+        lowE(1, 0)
+        lowQ(0)
+        iT(2)
+        lowE(1, 1)
+        lowE(2, 1)
+        iQ(0)
         lowE(2, 0)
         lowT(3, 1)
-        iE(2)
         sqT()
-        sP()
-        iT(3)
+        iE(1, 1)
         lowE(3, 0)
-        S2(1, 1, 0)
-        lowQ(2)
+        sP()
         lowE(3, 1)
-        S1(1, 0)
-        iE(3)
-        iQ(2)
+        S2(0, 0, 0)
+        wP(0)
+        E2(0, 0, 0)
+        wP(1)
+        S2(1, 0, 1)
+        iQ(1)
+        S2(0, 0, 1)
+        S1(0, 1)
+        lowQ(1)
+        S2(0, 1, 1)
+        lowQ(2)
+        S2(0, 1, 0)
+        sqE()
+        iE(3, 1)
+        lowQ(3)
+        E2(1, 0, 1)
+        S1(0, 0)
+        S2(0, 2, 0)
         fC(2)
+        S2(1, 2, 1)
+        iE(2, 1)
+        fQ(2)
+        S1(0, 2)
+        E1(0, 0)
+        E1(0, 1)
+        E2(0, 1, 1)
+        E2(0, 2, 0)
+        E2(1, 2, 1)
+        E2(0, 0, 1)
+        S2(1, 0, 0)
+        E1(0, 2)
+        S1(0, 3)
+        E2(0, 1, 0)
+        S2(0, 3, 1)
+        E2(0, 3, 1)
+        S2(0, 3, 0)
+        E1(0, 3)
+        S2(1, 3, 0)
+        iE(2, 0)
+        S2(1, 2, 0)
+        S2(1, 1, 1)
+        fC(3)
         S2(0, 2, 1)
         E2(1, 0, 0)
-        S1(0, 0)
-        iQ(3)
-        E2(0, 2, 1)
-        lowQ(3)
-        sqE()
-        S1(0, 2)
-        fC(3)
-        E1(0, 0)
-        S1(0, 1)
-        E1(0, 2)
-        S2(0, 3, 0)
-        S2(0, 3, 1)
-        E1(0, 1)
-        E2(0, 3, 0)
-        S1(0, 3)
-        fQ(2)
-        E2(0, 3, 1)
-        Q1(0, 0)
-        S2(0, 2, 0)
-        S2(2, 1, 1)
-        E1(0, 3)
-        E2(0, 2, 0)
-        S2(1, 2, 0)
-        E1(1, 0)
-        S1(1, 1)
-        E2(2, 1, 1)
-        Q1(0, 1)
+        Q2(0, 0)
         E2(1, 2, 0)
-        S1(1, 2)
-        E2(1, 1, 0)
-        S2(1, 3, 0)
-        E2(1, 1, 1)
-        S1(2, 2)
         E2(1, 3, 0)
-        Q2(0, 1)
-        S2(2, 0, 1)
-        Q2(1, 0)
-        S2(1, 3, 1)
-        E2(2, 0, 1)
-        S1(1, 3)
-        E1(2, 2)
-        E2(1, 3, 1)
+        E2(0, 3, 0)
+        S2(1, 1, 0)
+        Q1(0, 1)
+        E2(0, 2, 1)
+        Q1(0, 0)
+        S2(2, 1, 1)
+        E2(1, 1, 0)
         S2(2, 0, 0)
-        E1(1, 2)
-        S1(2, 0)
-        E2(2, 0, 0)
-        E1(1, 3)
-        S3(0, 0)
-        E1(1, 1)
-        S1(2, 1)
-        OV(0, 0)
-        Q1(1, 1)
-        Q1(1, 0)
-        S2(2, 2, 0)
-        E1(2, 0)
+        S1(1, 0)
+        S1(1, 1)
+        E1(1, 0)
+        E2(1, 1, 1)
         S2(2, 1, 0)
+        S2(2, 0, 1)
+        Q2(0, 1)
+        S1(1, 3)
+        S3(0, 0)
+        iQ(2)
+        S2(2, 2, 0)
+        fQ(3)
+        E1(1, 1)
+        iE(3, 0)
+        iQ(3)
+        E2(2, 0, 1)
+        E2(2, 1, 1)
+        OV(0, 0)
+        ST(0, 0)
+        S1(1, 2)
+        E1(1, 2)
+        E2(2, 0, 0)
+        S2(1, 3, 1)
+        E2(1, 3, 1)
+        S2(2, 3, 1)
+        E1(1, 3)
+        Q2(1, 0)
+        S1(2, 2)
+        Q1(1, 1)
+        S2(2, 2, 1)
+        S1(3, 0)
+        Q2(1, 1)
+        E1(2, 2)
+        S1(2, 1)
+        S1(2, 0)
+        Q1(1, 0)
         E2(2, 2, 0)
-        S3(1, 0)
+        S1(2, 3)
+        S2(2, 3, 0)
+        E2(2, 3, 1)
         E1(2, 1)
         E2(2, 1, 0)
-        S2(2, 2, 1)
-        ST(0, 0)
-        S2(2, 3, 1)
-        OV(1, 0)
-        Q2(2, 0)
-        S2(2, 3, 0)
-        E2(2, 2, 1)
-        S1(3, 0)
-        ST(1, 0)
-        E2(2, 3, 0)
-        Q1(2, 0)
-        S2(1, 2, 1)
-        E2(2, 3, 1)
-        E1(3, 0)
-        S1(3, 1)
-        E2(1, 2, 1)
-        fQ(3)
-        S1(2, 3)
-        Q2(2, 1)
-        S2(3, 3, 0)
-        Q2(1, 1)
-        S2(3, 0, 1)
-        S2(3, 0, 0)
-        E1(2, 3)
         S3(1, 1)
-        E2(3, 0, 0)
-        E2(3, 0, 1)
-        S3(0, 1)
+        Q2(2, 0)
+        S2(3, 0, 1)
+        E2(2, 3, 0)
         OV(1, 1)
+        S3(1, 0)
+        E1(2, 3)
+        S2(3, 1, 1)
+        E1(2, 0)
         Q1(2, 1)
         S2(3, 1, 0)
-        E2(3, 3, 0)
-        OV(0, 1)
-        S3(2, 1)
-        E2(3, 1, 0)
-        ST(0, 1)
-        S2(3, 1, 1)
         ST(1, 1)
-        OV(2, 1)
-        S2(3, 2, 0)
-        E1(3, 1)
+        E2(2, 2, 1)
+        OV(1, 0)
         E2(3, 1, 1)
+        Q2(2, 1)
+        Q1(2, 0)
+        E2(3, 0, 1)
+        S1(3, 1)
+        S1(3, 2)
+        ST(1, 0)
+        S2(3, 0, 0)
+        E2(3, 1, 0)
+        E1(3, 1)
+        E1(3, 0)
+        S3(0, 1)
+        E2(3, 0, 0)
+        OV(0, 1)
+        E1(3, 2)
         S3(0, 2)
-        ST(2, 1)
-        E2(3, 2, 0)
-        S2(3, 2, 1)
-        Q1(3, 0)
+        Q2(3, 0)
         S3(2, 0)
         OV(0, 2)
-        Q2(3, 0)
-        E2(3, 2, 1)
-        S1(3, 2)
         ST(0, 2)
         OV(2, 0)
+        S2(3, 2, 1)
+        S2(3, 3, 0)
+        E2(3, 3, 0)
+        ST(0, 1)
         S2(3, 3, 1)
-        E1(3, 2)
-        S3(1, 2)
-        E2(3, 3, 1)
+        S2(3, 2, 0)
         ST(2, 0)
+        E2(3, 2, 0)
         S1(3, 3)
+        E2(3, 3, 1)
+        S3(2, 1)
+        E2(3, 2, 1)
+        Q1(3, 0)
+        S3(1, 2)
+        E1(3, 3)
+        OV(2, 1)
         OV(1, 2)
         Q2(3, 1)
         S3(2, 2)
-        ST(1, 2)
         S3(0, 3)
-        E1(3, 3)
         OV(2, 2)
-        S3(1, 3)
-        ST(2, 2)
-        OV(0, 3)
         Q1(3, 1)
-        S3(2, 3)
-        ST(0, 3)
-        OV(1, 3)
-        S3(3, 1)
-        ST(1, 3)
-        OV(2, 3)
         S3(3, 0)
-        ST(2, 3)
-        OV(3, 1)
-        S3(3, 3)
-        ST(3, 1)
-        OV(3, 0)
+        S3(3, 1)
+        ST(2, 1)
+        ST(2, 2)
         S3(3, 2)
-        ST(3, 0)
-        OV(3, 3)
-        ST(3, 3)
+        OV(0, 3)
+        OV(3, 0)
+        ST(1, 2)
+        ST(0, 3)
+        OV(3, 1)
         OV(3, 2)
+        ST(3, 0)
+        S3(1, 3)
+        OV(1, 3)
+        ST(3, 1)
+        S3(2, 3)
         ST(3, 2)
+        OV(2, 3)
+        ST(1, 3)
+        S3(3, 3)
+        OV(3, 3)
+        ST(2, 3)
+        ST(3, 3)

@@ -63,20 +63,20 @@ def tile_franck_condon_overlap_table_s11_kernel(
         make_identity(nc, ident[:])
         make_identity(nc, identb[:])
         nc.sync.dma_start(out=ibytes[:, 0:2, :], in_=ib_v[:, 0:2, :])
-        nc.sync.dma_start(out=low_raw[0][:, 0:2, :], in_=low_v[0][:, 0:2, :])
-        nc.sync.dma_start(out=fin_raw[0][:], in_=fin_v[:, :, 0:512])
-        nc.sync.dma_start(out=low_raw[0][:, 2:4, :], in_=low_v[0][:, 2:4, :])
-        nc.sync.dma_start(out=low_raw[1][:], in_=low_v[1])
         nc.sync.dma_start(out=ibytes[:, 2:4, :], in_=ib_v[:, 2:4, :])
+        nc.sync.dma_start(out=fin_raw[0][:], in_=fin_v[:, :, 0:512])
+        nc.sync.dma_start(out=low_raw[0][:, 0:2, :], in_=low_v[0][:, 0:2, :])
+        nc.sync.dma_start(out=low_raw[1][:], in_=low_v[1])
+        nc.sync.dma_start(out=low_raw[0][:, 2:4, :], in_=low_v[0][:, 2:4, :])
         nc.sync.dma_start(out=low_raw[2][:], in_=low_v[2])
+        nc.sync.dma_start(out=low_raw[3][:], in_=low_v[3])
         for q in range(4):
             nc.sync.dma_start(
                 out=ws_raw[32 * q : 32 * q + 4, :, :].bitcast(I32),
                 in_=raising_scales[:, 4 * q : 4 * q + 4, :].rearrange("g q n -> q g n").bitcast(I32),
             )
-        nc.sync.dma_start(out=low_raw[3][:], in_=low_v[3])
-        nc.sync.dma_start(out=w_raw[0][:].bitcast(I32), in_=raising_words[0].bitcast(I32))
         nc.sync.dma_start(out=w_raw[1][:].bitcast(I32), in_=raising_words[1].bitcast(I32))
+        nc.sync.dma_start(out=w_raw[0][:].bitcast(I32), in_=raising_words[0].bitcast(I32))
         nc.sync.dma_start(out=fin_raw[1][:], in_=fin_v[:, :, 512:1024])
         for g in range(NG):
             nc.scalar.dma_start(
@@ -88,8 +88,8 @@ def tile_franck_condon_overlap_table_s11_kernel(
             out=perm[:].rearrange("p (t q h) -> p t q h", t=4, q=16), in_=ident[:].rearrange("p (q t h) -> p t q h", q=16, t=4)
         )
 
-        LOWE, IK, FC, WSPLIT = "SSSVSSSS", "VSSS", "SVSV", 1
-        E2V = [(3, 2, 1)]
+        LOWE, IK, FC, WSPLIT = "SSSSSSSS", "VVVS", "SSVV", 1
+        E2V = [(0, 2, 1),(2, 3, 0)]
         low_grp = [keep("low_grp%d" % g, [P, 2048], BF16) for g in range(NG)]
         low_q = [keep("low_q%d" % g, [P, 512], U32) for g in range(NG)]
         low_s = [keep("low_s%d" % g, [P, 512], U8) for g in range(NG)]
@@ -266,228 +266,238 @@ def tile_franck_condon_overlap_table_s11_kernel(
                     stop=(gg == NG - 1),
                 )
 
+        def store(dst, src, a, f):
+            if (a, f // 2) == (NA - 1, 1):
+                lo, hi = f, f + 1
+            elif f % 2 == 1:
+                lo, hi = f - 1, f + 1
+            else:
+                return
+            cols = slice(lo * FQ, hi * FQ)
+            nc.sync.dma_start(out=dst[:, a, cols], in_=src[:, a, cols])
+
         def OV(a, f):
             cols = slice(f * FQ, (f + 1) * FQ)
             nc.scalar.copy(out=ov[:, a, cols], in_=banks[("o", a, f)][:, 0:FQ])
-            nc.sync.dma_start(out=out0_v[:, a, cols], in_=ov[:, a, cols])
+            store(out0_v, ov, a, f)
 
         def ST(a, f):
             cols = slice(f * FQ, (f + 1) * FQ)
             nc.vector.scalar_tensor_tensor(
                 out=st[:, a, cols], in0=banks[("o", a, f)][:, 0:FQ], scalar=pop[:, a : a + 1], in1=ov[:, a, cols], op0=MULT, op1=MULT
             )
-            nc.sync.dma_start(out=out1_v[:, a, cols], in_=st[:, a, cols])
+            store(out1_v, st, a, f)
 
         iK(1)
-        fC(0)
-        lowT(0, 0)
+        iT(1)
         iK(0)
+        iK(3)
+        iK(2)
+        fC(0)
         iT(0)
+        iE(1, 1)
+        fC(1)
+        iE(0, 1)
+        iT(3)
+        lowT(0, 0)
+        iT(2)
+        lowT(1, 0)
+        lowT(1, 1)
         lowT(0, 1)
         lowE(0, 0)
-        iT(1)
-        lowE(0, 1)
-        lowT(1, 1)
-        lowT(1, 0)
         iE(0, 0)
-        iK(3)
-        fC(1)
-        fQ(1)
-        iE(1, 0)
-        fQ(0)
         lowT(2, 0)
-        iT(3)
-        iE(0, 1)
-        iK(2)
         lowT(2, 1)
         lowT(3, 0)
+        iE(1, 0)
+        fQ(0)
         lowE(1, 0)
-        lowQ(0)
-        iT(2)
-        lowE(1, 1)
-        lowE(2, 1)
-        iQ(0)
-        lowE(2, 0)
+        iE(2, 1)
         lowT(3, 1)
-        sqT()
-        iE(1, 1)
+        lowE(1, 1)
+        lowE(0, 1)
+        fQ(1)
+        iE(3, 0)
+        iE(2, 0)
+        lowE(2, 0)
+        iE(3, 1)
+        lowQ(0)
+        lowE(2, 1)
+        lowQ(1)
+        lowQ(2)
         lowE(3, 0)
         sP()
+        sqT()
         lowE(3, 1)
-        S2(0, 0, 0)
-        wP(0)
-        E2(0, 0, 0)
-        wP(1)
-        S2(1, 0, 1)
-        iQ(1)
-        S2(0, 0, 1)
-        S1(0, 1)
-        lowQ(1)
-        S2(0, 1, 1)
-        lowQ(2)
-        S2(0, 1, 0)
         sqE()
-        iE(3, 1)
         lowQ(3)
-        E2(1, 0, 1)
-        S1(0, 0)
-        S2(0, 2, 0)
-        fC(2)
-        S2(1, 2, 1)
-        iE(2, 1)
-        fQ(2)
-        S1(0, 2)
-        E1(0, 0)
-        E1(0, 1)
-        E2(0, 1, 1)
-        E2(0, 2, 0)
-        E2(1, 2, 1)
+        iQ(0)
+        wP(1)
+        wP(0)
+        iQ(3)
+        S2(0, 0, 0)
+        E2(0, 0, 0)
+        S2(0, 0, 1)
         E2(0, 0, 1)
-        S2(1, 0, 0)
-        E1(0, 2)
-        S1(0, 3)
+        S2(0, 1, 0)
         E2(0, 1, 0)
+        S2(0, 1, 1)
+        E2(0, 1, 1)
+        S2(0, 2, 0)
+        E2(0, 2, 0)
+        S2(0, 2, 1)
+        E2(0, 2, 1)
+        S2(0, 3, 0)
+        E2(0, 3, 0)
         S2(0, 3, 1)
         E2(0, 3, 1)
-        S2(0, 3, 0)
-        E1(0, 3)
-        S2(1, 3, 0)
-        iE(2, 0)
-        S2(1, 2, 0)
-        S2(1, 1, 1)
-        fC(3)
-        S2(0, 2, 1)
+        S2(1, 0, 0)
         E2(1, 0, 0)
-        Q2(0, 0)
-        E2(1, 2, 0)
-        E2(1, 3, 0)
-        E2(0, 3, 0)
+        S2(1, 0, 1)
+        E2(1, 0, 1)
         S2(1, 1, 0)
-        Q1(0, 1)
-        E2(0, 2, 1)
-        Q1(0, 0)
-        S2(2, 1, 1)
         E2(1, 1, 0)
-        S2(2, 0, 0)
-        S1(1, 0)
-        S1(1, 1)
-        E1(1, 0)
+        fC(2)
+        S1(0, 0)
+        E1(0, 0)
+        iQ(1)
+        fQ(2)
+        fC(3)
+        S2(1, 1, 1)
         E2(1, 1, 1)
-        S2(2, 1, 0)
-        S2(2, 0, 1)
+        S2(1, 2, 0)
+        E2(1, 2, 0)
+        S1(0, 1)
+        E1(0, 1)
+        Q2(0, 0)
         Q2(0, 1)
-        S1(1, 3)
-        S3(0, 0)
-        iQ(2)
-        S2(2, 2, 0)
-        fQ(3)
-        E1(1, 1)
-        iE(3, 0)
-        iQ(3)
-        E2(2, 0, 1)
-        E2(2, 1, 1)
-        OV(0, 0)
-        ST(0, 0)
-        S1(1, 2)
-        E1(1, 2)
-        E2(2, 0, 0)
+        S2(1, 2, 1)
+        E2(1, 2, 1)
+        S2(1, 3, 0)
+        E2(1, 3, 0)
+        S1(0, 2)
+        E1(0, 2)
+        Q2(1, 0)
+        Q1(0, 0)
         S2(1, 3, 1)
         E2(1, 3, 1)
-        S2(2, 3, 1)
-        E1(1, 3)
-        Q2(1, 0)
-        S1(2, 2)
-        Q1(1, 1)
-        S2(2, 2, 1)
-        S1(3, 0)
-        Q2(1, 1)
-        E1(2, 2)
-        S1(2, 1)
-        S1(2, 0)
-        Q1(1, 0)
-        E2(2, 2, 0)
-        S1(2, 3)
-        S2(2, 3, 0)
-        E2(2, 3, 1)
-        E1(2, 1)
+        S2(2, 0, 0)
+        E2(2, 0, 0)
+        S1(0, 3)
+        E1(0, 3)
+        fQ(3)
+        S2(2, 0, 1)
+        E2(2, 0, 1)
+        S2(2, 1, 0)
         E2(2, 1, 0)
-        S3(1, 1)
-        Q2(2, 0)
-        S2(3, 0, 1)
-        E2(2, 3, 0)
-        OV(1, 1)
-        S3(1, 0)
-        E1(2, 3)
-        S2(3, 1, 1)
-        E1(2, 0)
-        Q1(2, 1)
-        S2(3, 1, 0)
-        ST(1, 1)
+        S2(2, 1, 1)
+        E2(2, 1, 1)
+        S1(1, 0)
+        E1(1, 0)
+        Q2(1, 1)
+        Q1(0, 1)
+        iQ(2)
+        S2(2, 2, 0)
+        E2(2, 2, 0)
+        S2(2, 2, 1)
         E2(2, 2, 1)
-        OV(1, 0)
-        E2(3, 1, 1)
-        Q2(2, 1)
-        Q1(2, 0)
-        E2(3, 0, 1)
-        S1(3, 1)
-        S1(3, 2)
-        ST(1, 0)
+        S1(1, 1)
+        E1(1, 1)
+        Q2(2, 0)
+        S2(2, 3, 0)
+        E2(2, 3, 0)
+        S2(2, 3, 1)
+        E2(2, 3, 1)
+        S1(1, 2)
+        E1(1, 2)
+        Q1(1, 0)
         S2(3, 0, 0)
-        E2(3, 1, 0)
-        E1(3, 1)
-        E1(3, 0)
-        S3(0, 1)
         E2(3, 0, 0)
+        S2(3, 0, 1)
+        E2(3, 0, 1)
+        S3(0, 0)
+        OV(0, 0)
+        S1(1, 3)
+        E1(1, 3)
+        Q2(2, 1)
+        ST(0, 0)
+        S2(3, 1, 0)
+        E2(3, 1, 0)
+        S2(3, 1, 1)
+        E2(3, 1, 1)
+        S2(3, 2, 0)
+        E2(3, 2, 0)
+        S3(0, 1)
         OV(0, 1)
-        E1(3, 2)
-        S3(0, 2)
-        Q2(3, 0)
-        S3(2, 0)
-        OV(0, 2)
-        ST(0, 2)
-        OV(2, 0)
+        S1(2, 0)
+        E1(2, 0)
+        Q1(1, 1)
+        ST(0, 1)
         S2(3, 2, 1)
+        E2(3, 2, 1)
         S2(3, 3, 0)
         E2(3, 3, 0)
-        ST(0, 1)
+        S3(0, 2)
+        OV(0, 2)
+        S1(2, 1)
+        E1(2, 1)
+        Q2(3, 0)
+        ST(0, 2)
         S2(3, 3, 1)
-        S2(3, 2, 0)
-        ST(2, 0)
-        E2(3, 2, 0)
-        S1(3, 3)
         E2(3, 3, 1)
-        S3(2, 1)
-        E2(3, 2, 1)
-        Q1(3, 0)
-        S3(1, 2)
-        E1(3, 3)
-        OV(2, 1)
-        OV(1, 2)
+        S1(2, 2)
+        E1(2, 2)
+        Q1(2, 0)
+        S3(1, 0)
+        OV(1, 0)
+        S1(2, 3)
+        E1(2, 3)
         Q2(3, 1)
-        S3(2, 2)
-        S3(0, 3)
-        OV(2, 2)
-        Q1(3, 1)
-        S3(3, 0)
-        S3(3, 1)
-        ST(2, 1)
-        ST(2, 2)
-        S3(3, 2)
-        OV(0, 3)
-        OV(3, 0)
+        ST(1, 0)
+        S3(1, 1)
+        OV(1, 1)
+        S1(3, 0)
+        E1(3, 0)
+        Q1(2, 1)
+        ST(1, 1)
+        S3(1, 2)
+        OV(1, 2)
+        S1(3, 1)
+        E1(3, 1)
         ST(1, 2)
+        S3(0, 3)
+        OV(0, 3)
+        S1(3, 2)
+        E1(3, 2)
+        Q1(3, 0)
         ST(0, 3)
-        OV(3, 1)
-        OV(3, 2)
-        ST(3, 0)
         S3(1, 3)
         OV(1, 3)
-        ST(3, 1)
-        S3(2, 3)
-        ST(3, 2)
-        OV(2, 3)
+        S1(3, 3)
+        E1(3, 3)
         ST(1, 3)
+        S3(2, 0)
+        OV(2, 0)
+        Q1(3, 1)
+        ST(2, 0)
+        S3(2, 1)
+        OV(2, 1)
+        ST(2, 1)
+        S3(2, 2)
+        OV(2, 2)
+        ST(2, 2)
+        S3(2, 3)
+        OV(2, 3)
+        ST(2, 3)
+        S3(3, 0)
+        OV(3, 0)
+        ST(3, 0)
+        S3(3, 1)
+        OV(3, 1)
+        ST(3, 1)
+        S3(3, 2)
+        OV(3, 2)
+        ST(3, 2)
         S3(3, 3)
         OV(3, 3)
-        ST(2, 3)
         ST(3, 3)

@@ -17,10 +17,23 @@ FP4X4 = mybir.dt.float4_e2m1fn_x4
 MULT = mybir.AluOpType.mult
 
 P = 128
+T = 4
+PASS = P * T
+KP = B // PASS
 NA = I // P
-NG = G // 512
-NQ = 4
-FQ = F // NQ
+NG = G // PASS
+NF = 4
+FQ = F // NF
+BANK = 512
+RUN = 8
+
+LEAD = 11
+UNITS_PER_STEP = 2.25
+WAIT = 3
+RIGHT_ON_VECTOR = (LEAD - 1,)
+WIDEN_ON_SCALAR = (3,)
+INTERLEAVE_ON_VECTOR = (2, 3)
+STORED_IN_HALVES = ((2, 0), (2, 1), (3, 0))
 
 
 def tile_franck_condon_overlap_table_s11_kernel(
@@ -28,476 +41,349 @@ def tile_franck_condon_overlap_table_s11_kernel(
 ):
     nc = tc.nc
     with ExitStack() as ctx:
-        sb = ctx.enter_context(tc.tile_pool(name="sb", bufs=1))
-        ps = ctx.enter_context(tc.psum_pool(name="ps", bufs=8))
+        sbuf = ctx.enter_context(tc.tile_pool(name="sbuf", bufs=1))
+        psum = ctx.enter_context(tc.psum_pool(name="psum", bufs=8))
 
         def keep(name, shape, dtype):
-            t = sb.tile(shape, dtype, name=name, tag=name, align_bytes=256)
-            return t
+            kept = sbuf.tile(shape, dtype, name=name, tag=name, align_bytes=256)
+            return kept
 
-        def bank(name, dtype=F32):
-            t = ps.tile([P, 512], dtype, name=name, tag="bank")
-            return t
+        def bank(dtype=F32):
+            taken = psum.tile([P, BANK], dtype, name="bank", tag="bank")
+            return taken
 
-        sc = keep("sc", [P, 2, 4], F32)
-        ibytes = keep("ibytes", [P, NA, B], U8)
-        low_raw = [keep("low_raw%d" % g, [P, 4, C], BF16) for g in range(NG)]
-        fin_raw = [keep("fin_raw%d" % h, [P, 4, 512], BF16) for h in range(2)]
-        w_raw = [keep("w_raw%d" % g, [P, 2 * G], U8) for g in range(2)]
-        ws_raw = keep("ws_raw", [P, 2, G], U8)
-        sq_rows = keep("sq_rows", [P, P], BF16)
-        pop = keep("pop", [P, NA], BF16)
-        ident = keep("ident", [P, P], F32)
-        identb = keep("identb", [P, P], BF16)
-        perm = keep("perm", [P, P], F32)
-        warm = keep("warm", [P, 1], F32)
+        def copy(on_vector, out, in_):
+            if on_vector:
+                nc.vector.tensor_copy(out=out, in_=in_)
+            else:
+                nc.scalar.copy(out=out, in_=in_)
+
         ctx.enter_context(tc.manual_schedule())
-        low_v = lowering.rearrange("(g p t) c -> g p t c", p=P, t=4)
-        ib_v = initial_bytes.rearrange("(p a) k -> p a k", a=NA)
-        fin_v = final.rearrange("(p j) f -> p j f", j=4)
-        nc.vector.memset(ws_raw[:].rearrange("p g n -> p (g n)").bitcast(I32), 0)
-        nc.vector.memset(sq_rows[:], 0.0)
-        nc.vector.memset(warm[:], 0.0)
-        nc.scalar.dma_start(out=sc[:], in_=initial_scale.rearrange("o (g p t) -> p (o g) t", p=P, t=4))
-        nc.scalar.copy(out=warm[:], in_=warm[:])
-        make_identity(nc, ident[:])
-        make_identity(nc, identb[:])
-        nc.sync.dma_start(out=ibytes[:, 0:2, :], in_=ib_v[:, 0:2, :])
-        nc.sync.dma_start(out=ibytes[:, 2:4, :], in_=ib_v[:, 2:4, :])
-        nc.sync.dma_start(out=fin_raw[0][:], in_=fin_v[:, :, 0:512])
-        nc.sync.dma_start(out=low_raw[0][:, 0:2, :], in_=low_v[0][:, 0:2, :])
-        nc.sync.dma_start(out=low_raw[1][:], in_=low_v[1])
-        nc.sync.dma_start(out=low_raw[0][:, 2:4, :], in_=low_v[0][:, 2:4, :])
-        nc.sync.dma_start(out=low_raw[2][:], in_=low_v[2])
-        nc.sync.dma_start(out=low_raw[3][:], in_=low_v[3])
-        for q in range(4):
+
+        bytes_in = keep("bytes_in", [P, NA, B], U8)
+        k_scale = keep("k_scale", [P, KP, T], F32)
+        low_rows = [keep("low_rows%d" % g, [P, T, C], BF16) for g in range(NG)]
+        fin_rows = [keep("fin_rows%d" % h, [P, T, F // 2], BF16) for h in range(2)]
+        words_in = [keep("words_in%d" % g, [P, 2 * G], U8) for g in range(KP)]
+        scales_in = keep("scales_in", [P, KP, G], U8)
+        squeeze_rows = keep("squeeze_rows", [P, P], BF16)
+        pop = keep("pop", [P, NA], BF16)
+        ident_f32 = keep("ident_f32", [P, P], F32)
+        ident_bf16 = keep("ident_bf16", [P, P], BF16)
+        by_slot = keep("by_slot", [P, P], F32)
+        table_load = keep("table_load", [P, 1], F32)
+
+        nc.vector.memset(scales_in[:].rearrange("p g n -> p (g n)").bitcast(I32), 0)
+        nc.vector.memset(squeeze_rows[:], 0.0)
+        nc.vector.memset(table_load[:], 0.0)
+        nc.scalar.dma_start(out=k_scale[:], in_=initial_scale.rearrange("o (g p t) -> p (o g) t", p=P, t=T))
+        nc.scalar.copy(out=table_load[:], in_=table_load[:])
+        make_identity(nc, ident_f32[:])
+        make_identity(nc, ident_bf16[:])
+
+        states = initial_bytes.rearrange("(m a) k -> m a k", a=NA)
+        low_groups = lowering.rearrange("(g m s) c -> g m s c", m=P, s=T)
+        fin_passes = final.rearrange("(p t) f -> p t f", t=T)
+        for h in range(2):
+            nc.sync.dma_start(out=bytes_in[:, 2 * h : 2 * h + 2, :], in_=states[:, 2 * h : 2 * h + 2, :])
+        nc.sync.dma_start(out=fin_rows[0][:], in_=fin_passes[:, :, : F // 2])
+        for g in range(NG):
+            nc.sync.dma_start(out=low_rows[g][:], in_=low_groups[g])
+        nc.sync.dma_start(out=words_in[0][:].bitcast(I32), in_=raising_words[0].bitcast(I32))
+        for quad in range(4):
             nc.sync.dma_start(
-                out=ws_raw[32 * q : 32 * q + 4, :, :].bitcast(I32),
-                in_=raising_scales[:, 4 * q : 4 * q + 4, :].rearrange("g q n -> q g n").bitcast(I32),
+                out=scales_in[32 * quad : 32 * quad + 4, :, :].bitcast(I32),
+                in_=raising_scales[:, 4 * quad : 4 * quad + 4, :].rearrange("g row n -> row g n").bitcast(I32),
             )
-        nc.sync.dma_start(out=w_raw[1][:].bitcast(I32), in_=raising_words[1].bitcast(I32))
-        nc.sync.dma_start(out=w_raw[0][:].bitcast(I32), in_=raising_words[0].bitcast(I32))
-        nc.sync.dma_start(out=fin_raw[1][:], in_=fin_v[:, :, 512:1024])
+        nc.sync.dma_start(out=words_in[1][:].bitcast(I32), in_=raising_words[1].bitcast(I32))
+        nc.sync.dma_start(out=fin_rows[1][:], in_=fin_passes[:, :, F // 2 :])
         for g in range(NG):
             nc.scalar.dma_start(
-                out=sq_rows[4 * g : 4 * g + 4, :].rearrange("t (q r) -> t q r", r=8),
-                in_=squeeze[512 * g : 512 * g + 512].rearrange("(q t r) -> t q r", q=16, t=4),
+                out=squeeze_rows[T * g : T * g + T, :].rearrange("t (q r) -> t q r", r=RUN),
+                in_=squeeze[PASS * g : PASS * (g + 1)].rearrange("(q t r) -> t q r", t=T, r=RUN),
             )
-        nc.scalar.dma_start(out=pop[:], in_=population.rearrange("(p a) -> p a", a=NA))
+        nc.scalar.dma_start(out=pop[:], in_=population.rearrange("(m a) -> m a", a=NA))
+
         nc.vector.tensor_copy(
-            out=perm[:].rearrange("p (t q h) -> p t q h", t=4, q=16), in_=ident[:].rearrange("p (q t h) -> p t q h", q=16, t=4)
+            out=by_slot[:].rearrange("p (t q h) -> p t q h", t=T, h=2),
+            in_=ident_f32[:].rearrange("p (q t h) -> p t q h", t=T, h=2),
         )
 
-        LOWE, IK, FC, WSPLIT = "SSSSSSSS", "VVVS", "SSVV", 1
-        E2V = [(0, 2, 1),(2, 3, 0)]
-        low_grp = [keep("low_grp%d" % g, [P, 2048], BF16) for g in range(NG)]
-        low_q = [keep("low_q%d" % g, [P, 512], U32) for g in range(NG)]
-        low_s = [keep("low_s%d" % g, [P, 512], U8) for g in range(NG)]
-        ini = keep("ini", [P, NA, B], BF16)
-        ini_grp = [keep("ini_grp%d" % a, [P, 1024], BF16) for a in range(NA)]
-        ini_q = [keep("ini_q%d" % a, [P, 256], U32) for a in range(NA)]
-        ini_s = [keep("ini_s%d" % a, [P, 256], U8) for a in range(NA)]
-        fin_grp = [keep("fin_grp%d" % f, [P, 1024], BF16) for f in range(NQ)]
-        fin_q = [keep("fin_q%d" % f, [P, FQ], U32) for f in range(NQ)]
-        fin_s = [keep("fin_s%d" % f, [P, FQ], U8) for f in range(NQ)]
-        w_q = [keep("w_q%d" % g, [P, 2 * G], U8) for g in range(2)]
-        w_s = keep("w_s", [P, 2, G], U8)
-        sq = keep("sq", [P, 16], F32)
-        left_grp = [keep("left_grp%d" % a, [P, NG * 512], BF16) for a in range(NA)]
-        left_q = [keep("left_q%d" % a, [P, NG * P], U32) for a in range(NA)]
-        left_s = [keep("left_s%d" % a, [P, NG * P], U8) for a in range(NA)]
-        right_grp = {}
-        right_q = [keep("right_q%d" % f, [P, NG * FQ], U32) for f in range(NQ)]
-        right_s = [keep("right_s%d" % f, [P, NG * FQ], U8) for f in range(NQ)]
-        ov = keep("ov", [P, NA, F], F32)
-        st = keep("st", [P, NA, F], F32)
-        out0_v = out_0.rearrange("(p a) f -> p a f", a=NA)
-        out1_v = out_1.rearrange("(p a) f -> p a f", a=NA)
-        banks = {}
+        ini_bf16 = keep("ini_bf16", [P, NA, B], BF16)
+        ini_grouped = [keep("ini_grouped%d" % a, [P, KP * P * T], BF16) for a in range(NA)]
+        ini_codes = [keep("ini_codes%d" % a, [P, KP * P], U32) for a in range(NA)]
+        ini_scales = [keep("ini_scales%d" % a, [P, KP * P], U8) for a in range(NA)]
+        low_grouped = [keep("low_grouped%d" % g, [P, PASS * T], BF16) for g in range(NG)]
+        low_codes = [keep("low_codes%d" % g, [P, PASS], U32) for g in range(NG)]
+        low_scales = [keep("low_scales%d" % g, [P, PASS], U8) for g in range(NG)]
+        fin_grouped = [keep("fin_grouped%d" % f, [P, FQ * T], BF16) for f in range(NF)]
+        fin_codes = [keep("fin_codes%d" % f, [P, FQ], U32) for f in range(NF)]
+        fin_scales = [keep("fin_scales%d" % f, [P, FQ], U8) for f in range(NF)]
+        words = [keep("words%d" % g, [P, 2 * G], U8) for g in range(KP)]
+        scales = keep("scales", [P, KP, G], U8)
+        squeeze_by_slot = keep("squeeze_by_slot", [P, NG * T], F32)
+        left_grouped = [keep("left_grouped%d" % a, [P, NG * P * T], BF16) for a in range(NA)]
+        left_codes = [keep("left_codes%d" % a, [P, NG * P], U32) for a in range(NA)]
+        left_scales = [keep("left_scales%d" % a, [P, NG * P], U8) for a in range(NA)]
+        right_grouped = [
+            sbuf.tile([P, NG * FQ * T], BF16, name="right_grouped%d" % f, tag="right_grouped", bufs=2, align_bytes=256)
+            for f in range(NF)
+        ]
+        right_codes = [keep("right_codes%d" % f, [P, NG * FQ], U32) for f in range(NF)]
+        right_scales = [keep("right_scales%d" % f, [P, NG * FQ], U8) for f in range(NF)]
+        overlap = keep("overlap", [P, NA, F], F32)
+        strength = keep("strength", [P, NA, F], F32)
 
-        def copy(eng, out, in_):
-            if eng == "S":
-                nc.scalar.copy(out=out, in_=in_)
-            else:
-                nc.vector.tensor_copy(out=out, in_=in_)
+        ini_banks = {}
 
-        def lowT(g, h):
-            words = low_raw[g][:].rearrange("p t c -> p (t c)").bitcast(F32)
-            xt = bank("xt")
-            banks[("x", g, h)] = xt
-            for x in range(4):
-                rl, u = 2 * h + x // 2, x % 2
-                nc.tensor.transpose(xt[:, x * P : (x + 1) * P], words[:, 256 * rl + u : 256 * (rl + 1) : 2], perm[:])
+        def widen_initial(a):
+            copy(a not in WIDEN_ON_SCALAR, ini_bf16[:, a, :], bytes_in[:, a, :].bitcast(FP8))
 
-        def lowE(g, h):
-            dst = low_grp[g][:].bitcast(F32).rearrange("p (j x) -> p j x", x=8)
-            copy(LOWE[2 * g + h], dst[:, :, 4 * h : 4 * h + 4], banks[("x", g, h)][:].rearrange("p (x j) -> p j x", x=4))
-
-        def lowQ(g):
-            nc.vector.quantize_mx(out=low_q[g][:].bitcast(FP8X4), scales=low_s[g][:], in_=low_grp[g][:])
-
-        def iK(a):
-            src = ibytes[:, a, :].bitcast(FP8)
-            if IK[a] == "V":
-                nc.vector.tensor_copy(out=ini[:, a, :], in_=src)
-            else:
-                nc.scalar.copy(out=ini[:, a, :], in_=src)
-
-        def iT(a):
-            words = ini[:, a, :].bitcast(F32)
-            xt = bank("xt")
-            banks[("y", a)] = xt
-            for g in range(2):
+        def transpose_initial(a):
+            pairs = ini_bf16[:, a, :].bitcast(F32)
+            ini_banks[a] = bank()
+            for g in range(KP):
                 for u in range(2):
-                    x = 2 * g + u
-                    nc.tensor.transpose(xt[:, x * P : (x + 1) * P], words[:, 256 * g + u : 256 * (g + 1) : 2], ident[:])
+                    at = (2 * g + u) * P
+                    every_second = slice(PASS // 2 * g + u, PASS // 2 * (g + 1), 2)
+                    nc.tensor.transpose(ini_banks[a][:, at : at + P], pairs[:, every_second], ident_f32[:])
 
-        def iE(a, g):
-            codes = banks[("y", a)][:, 256 * g : 256 * (g + 1)].bitcast(BF16)
+        def scale_initial(a, g):
+            pairs = ini_banks[a][:, 2 * P * g : 2 * P * (g + 1)].bitcast(BF16)
             nc.vector.tensor_tensor(
-                out=ini_grp[a][:, 512 * g : 512 * (g + 1)].rearrange("p (m u e) -> p m u e", u=2, e=2),
-                in0=codes.rearrange("p (u m e) -> p m u e", u=2, e=2),
-                in1=sc[:, g, :].rearrange("p (u e) -> p u e", u=2).unsqueeze(1).to_broadcast([P, P, 2, 2]),
+                out=ini_grouped[a][:, P * T * g : P * T * (g + 1)].rearrange("p (m u e) -> p m u e", u=2, e=2),
+                in0=pairs.rearrange("p (u m e) -> p m u e", u=2, e=2),
+                in1=k_scale[:, g, :].rearrange("p (u e) -> p u e", u=2).unsqueeze(1).to_broadcast([P, P, 2, 2]),
                 op=MULT,
             )
 
-        def iQ(a):
-            nc.vector.quantize_mx(out=ini_q[a][:].bitcast(FP8X4), scales=ini_s[a][:], in_=ini_grp[a][:])
+        def quantise_initial(a):
+            nc.vector.quantize_mx(out=ini_codes[a][:].bitcast(FP8X4), scales=ini_scales[a][:], in_=ini_grouped[a][:])
 
-        def fC(f):
-            cols = slice((f % 2) * FQ, (f % 2) * FQ + FQ)
-            copy(FC[f], fin_grp[f][:].rearrange("p (f j) -> p f j", j=4), fin_raw[f // 2][:, :, cols].rearrange("p j f -> p f j"))
+        def interleave_final(f):
+            cols = slice(FQ * (f % 2), FQ * (f % 2 + 1))
+            copy(
+                f in INTERLEAVE_ON_VECTOR,
+                fin_grouped[f][:].rearrange("p (n i t) -> p n t i", i=4, t=T),
+                fin_rows[f // 2][:, :, cols].rearrange("p t (n i) -> p n t i", i=4),
+            )
 
-        def fQ(f):
-            nc.vector.quantize_mx(out=fin_q[f][:].bitcast(FP8X4), scales=fin_s[f][:], in_=fin_grp[f][:])
+        def quantise_final(f):
+            nc.vector.quantize_mx(out=fin_codes[f][:].bitcast(FP8X4), scales=fin_scales[f][:], in_=fin_grouped[f][:])
 
-        def wP(g):
-            for h in range(WSPLIT):
-                n = 4096 // WSPLIT
-                cols = slice(n * h, n * (h + 1))
+        low_banks = {}
+
+        def transpose_lowering(g, half):
+            pairs = low_rows[g][:].rearrange("m s c -> m (s c)").bitcast(F32)
+            low_banks[(g, half)] = bank()
+            for x in range(4):
+                s, u = 2 * half + x // 2, x % 2
+                every_second = slice(C // 2 * s + u, C // 2 * (s + 1), 2)
+                nc.tensor.transpose(low_banks[(g, half)][:, x * P : (x + 1) * P], pairs[:, every_second], by_slot[:])
+
+        def group_lowering(g, half):
+            by_column = low_grouped[g][:].bitcast(F32).rearrange("p (j x) -> p j x", x=8)
+            copy(False, by_column[:, :, 4 * half : 4 * half + 4], low_banks[(g, half)][:].rearrange("p (x j) -> p j x", x=4))
+
+        def quantise_lowering(g):
+            nc.vector.quantize_mx(out=low_codes[g][:].bitcast(FP8X4), scales=low_scales[g][:], in_=low_grouped[g][:])
+
+        def move_words(g):
+            nc.vector.tensor_copy(
+                out=words[g][:].bitcast(I32).rearrange("p (n t q w) -> p n t q w", n=NG, t=T, w=RUN // 2),
+                in_=words_in[g][:].bitcast(I32).rearrange("p (n q t w) -> p n t q w", n=NG, t=T, w=RUN // 2),
+            )
+
+        def move_scales():
+            for g in range(KP):
                 nc.vector.tensor_copy(
-                    out=w_q[g][:, cols].bitcast(I32).rearrange("p (b t q w) -> p b t q w", t=4, q=16, w=4),
-                    in_=w_raw[g][:, cols].bitcast(I32).rearrange("p (b q t w) -> p b t q w", t=4, q=16, w=4),
+                    out=scales[:, g, :].bitcast(I32).rearrange("p (n t q w) -> p n t q w", n=NG, t=T, w=RUN // 4),
+                    in_=scales_in[:, g, :].bitcast(I32).rearrange("p (n q t w) -> p n t q w", n=NG, t=T, w=RUN // 4),
                 )
 
-        def sP():
-            for g in range(2):
-                nc.vector.tensor_copy(
-                    out=w_s[:, g, :].bitcast(I32).rearrange("p (b t q w) -> p b t q w", t=4, q=16, w=2),
-                    in_=ws_raw[:, g, :].bitcast(I32).rearrange("p (b q t w) -> p b t q w", t=4, q=16, w=2),
-                )
+        def spread_squeeze():
+            turned = bank(BF16)
+            nc.tensor.transpose(turned[:, :P], squeeze_rows[:], ident_bf16[:])
+            nc.vector.tensor_copy(out=squeeze_by_slot[:], in_=turned[:, : NG * T])
 
-        def sqT():
-            banks["sq"] = bank("sqt", BF16)
-            nc.tensor.transpose(banks["sq"][:, 0:P], sq_rows[:], identb[:])
-
-        def sqE():
-            nc.vector.tensor_copy(out=sq[:], in_=banks["sq"][:, 0:16])
-
-        def S1(a, gg):
-            acc = bank("acc")
-            banks[("l", a, gg)] = acc
-            for t in range(4):
-                j = 4 * gg + t
-                for g in range(2):
+        def left_step(a, g):
+            sums = bank()
+            for t in range(T):
+                slot = slice(P * (T * g + t), P * (T * g + t + 1))
+                for k in range(KP):
                     nc.tensor.matmul_mx(
-                        out=acc[:, t * P : (t + 1) * P],
-                        lhsT=w_q[g][:, 256 * j : 256 * (j + 1)].bitcast(FP4X4),
-                        lhsT_scale=w_s[:, g, P * j : P * (j + 1)],
-                        rhs=ini_q[a][:, g * P : (g + 1) * P].bitcast(FP8X4),
-                        rhs_scale=ini_s[a][:, g * P : (g + 1) * P],
-                        start=(g == 0),
-                        stop=(g == 1),
+                        out=sums[:, P * t : P * (t + 1)],
+                        lhsT=words[k][:, 2 * slot.start : 2 * slot.stop].bitcast(FP4X4),
+                        lhsT_scale=scales[:, k, slot],
+                        rhs=ini_codes[a][:, P * k : P * (k + 1)].bitcast(FP8X4),
+                        rhs_scale=ini_scales[a][:, P * k : P * (k + 1)],
+                        start=(k == 0),
+                        stop=(k == KP - 1),
                     )
-
-        def E1(a, gg):
             nc.vector.tensor_tensor(
-                out=left_grp[a][:, 512 * gg : 512 * (gg + 1)].rearrange("p (m t) -> p m t", t=4),
-                in0=banks[("l", a, gg)][:].rearrange("p (t m) -> p m t", t=4),
-                in1=sq[:, 4 * gg : 4 * gg + 4].unsqueeze(1).to_broadcast([P, P, 4]),
+                out=left_grouped[a][:, P * T * g : P * T * (g + 1)].rearrange("p (m t) -> p m t", t=T),
+                in0=sums[:].rearrange("p (t m) -> p m t", t=T),
+                in1=squeeze_by_slot[:, T * g : T * (g + 1)].unsqueeze(1).to_broadcast([P, P, T]),
                 op=MULT,
             )
 
-        def Q1(a, h):
+        def quantise_left(a, pair):
+            cols = slice(2 * P * pair, 2 * P * (pair + 1))
             nc.vector.quantize_mx(
-                out=left_q[a][:, 256 * h : 256 * (h + 1)].bitcast(FP8X4),
-                scales=left_s[a][:, 256 * h : 256 * (h + 1)],
-                in_=left_grp[a][:, 1024 * h : 1024 * (h + 1)],
+                out=left_codes[a][:, cols].bitcast(FP8X4),
+                scales=left_scales[a][:, cols],
+                in_=left_grouped[a][:, T * cols.start : T * cols.stop],
             )
 
-        def S2(f, gg, c):
-            acc = bank("acc")
-            banks[("r", f, gg, c)] = acc
-            for t in range(4):
+        units = [(f, g, half) for f in range(NF) for g in range(NG) for half in range(2)]
+
+        def right_unit(number):
+            f, g, half = units[number]
+            cols = slice(P * half, P * (half + 1))
+            sums = bank()
+            for t in range(T):
+                slot = slice(P * t, P * (t + 1))
                 nc.tensor.matmul_mx(
-                    out=acc[:, t * P : (t + 1) * P],
-                    lhsT=low_q[gg][:, t * P : (t + 1) * P].bitcast(FP8X4),
-                    lhsT_scale=low_s[gg][:, t * P : (t + 1) * P],
-                    rhs=fin_q[f][:, c * P : (c + 1) * P].bitcast(FP8X4),
-                    rhs_scale=fin_s[f][:, c * P : (c + 1) * P],
+                    out=sums[:, slot],
+                    lhsT=low_codes[g][:, slot].bitcast(FP8X4),
+                    lhsT_scale=low_scales[g][:, slot],
+                    rhs=fin_codes[f][:, cols].bitcast(FP8X4),
+                    rhs_scale=fin_scales[f][:, cols],
                     start=True,
                     stop=True,
                 )
-
-        def E2(f, gg, c):
-            if f not in right_grp:
-                right_grp[f] = sb.tile([P, NG * 4 * FQ], BF16, name="right_grp%d" % f, tag="right_grp", bufs=2, align_bytes=256)
-            dst = right_grp[f][:, 1024 * gg + 512 * c : 1024 * gg + 512 * (c + 1)].rearrange("p (f t) -> p f t", t=4)
-            copy("V" if (f, gg, c) in E2V else "S", dst, banks[("r", f, gg, c)][:].rearrange("p (t f) -> p f t", t=4))
-
-        def Q2(f, h):
-            nc.vector.quantize_mx(
-                out=right_q[f][:, 512 * h : 512 * (h + 1)].bitcast(FP8X4),
-                scales=right_s[f][:, 512 * h : 512 * (h + 1)],
-                in_=right_grp[f][:, 2048 * h : 2048 * (h + 1)],
+            at = T * (FQ * g + P * half)
+            copy(
+                number in RIGHT_ON_VECTOR,
+                right_grouped[f][:, at : at + T * P].rearrange("p (n t) -> p n t", t=T),
+                sums[:].rearrange("p (t n) -> p n t", t=T),
             )
 
-        def S3(a, f):
-            acc = bank("acc")
-            banks[("o", a, f)] = acc
-            for gg in range(NG):
-                nc.tensor.matmul_mx(
-                    out=acc[:, 0:FQ],
-                    lhsT=left_q[a][:, gg * P : (gg + 1) * P].bitcast(FP8X4),
-                    lhsT_scale=left_s[a][:, gg * P : (gg + 1) * P],
-                    rhs=right_q[f][:, gg * FQ : (gg + 1) * FQ].bitcast(FP8X4),
-                    rhs_scale=right_s[f][:, gg * FQ : (gg + 1) * FQ],
-                    start=(gg == 0),
-                    stop=(gg == NG - 1),
-                )
+        def quantise_right(f, pair):
+            cols = slice(2 * FQ * pair, 2 * FQ * (pair + 1))
+            nc.vector.quantize_mx(
+                out=right_codes[f][:, cols].bitcast(FP8X4),
+                scales=right_scales[f][:, cols],
+                in_=right_grouped[f][:, T * cols.start : T * cols.stop],
+            )
 
-        def store(dst, src, a, f):
-            if (a, f // 2) == (NA - 1, 1):
-                lo, hi = f, f + 1
+        overlap_banks = {}
+
+        def store(out, made, a, f):
+            if (a, f // 2) not in STORED_IN_HALVES:
+                cols = slice(FQ * f, FQ * (f + 1))
             elif f % 2 == 1:
-                lo, hi = f - 1, f + 1
+                cols = slice(FQ * (f - 1), FQ * (f + 1))
             else:
                 return
-            cols = slice(lo * FQ, hi * FQ)
-            nc.sync.dma_start(out=dst[:, a, cols], in_=src[:, a, cols])
+            nc.sync.dma_start(out=out.rearrange("(m a) f -> m a f", a=NA)[:, a, cols], in_=made[:, a, cols])
 
-        def OV(a, f):
-            cols = slice(f * FQ, (f + 1) * FQ)
-            nc.scalar.copy(out=ov[:, a, cols], in_=banks[("o", a, f)][:, 0:FQ])
-            store(out0_v, ov, a, f)
+        def make_overlap(a, f):
+            sums = bank()
+            overlap_banks[(a, f)] = sums
+            for g in range(NG):
+                nc.tensor.matmul_mx(
+                    out=sums[:, :FQ],
+                    lhsT=left_codes[a][:, P * g : P * (g + 1)].bitcast(FP8X4),
+                    lhsT_scale=left_scales[a][:, P * g : P * (g + 1)],
+                    rhs=right_codes[f][:, FQ * g : FQ * (g + 1)].bitcast(FP8X4),
+                    rhs_scale=right_scales[f][:, FQ * g : FQ * (g + 1)],
+                    start=(g == 0),
+                    stop=(g == NG - 1),
+                )
+            nc.scalar.copy(out=overlap[:, a, FQ * f : FQ * (f + 1)], in_=sums[:, :FQ])
+            store(out_0, overlap, a, f)
 
-        def ST(a, f):
-            cols = slice(f * FQ, (f + 1) * FQ)
+        def make_strength(a, f):
+            cols = slice(FQ * f, FQ * (f + 1))
             nc.vector.scalar_tensor_tensor(
-                out=st[:, a, cols], in0=banks[("o", a, f)][:, 0:FQ], scalar=pop[:, a : a + 1], in1=ov[:, a, cols], op0=MULT, op1=MULT
+                out=strength[:, a, cols],
+                in0=overlap_banks[(a, f)][:, :FQ],
+                scalar=pop[:, a : a + 1],
+                in1=overlap[:, a, cols],
+                op0=MULT,
+                op1=MULT,
             )
-            store(out1_v, st, a, f)
+            store(out_1, strength, a, f)
 
-        iK(1)
-        iT(1)
-        iK(0)
-        iK(3)
-        iK(2)
-        fC(0)
-        iT(0)
-        iE(1, 1)
-        fC(1)
-        iE(0, 1)
-        iT(3)
-        lowT(0, 0)
-        iT(2)
-        lowT(1, 0)
-        lowT(1, 1)
-        lowT(0, 1)
-        lowE(0, 0)
-        iE(0, 0)
-        lowT(2, 0)
-        lowT(2, 1)
-        lowT(3, 0)
-        iE(1, 0)
-        fQ(0)
-        lowE(1, 0)
-        iE(2, 1)
-        lowT(3, 1)
-        lowE(1, 1)
-        lowE(0, 1)
-        fQ(1)
-        iE(3, 0)
-        iE(2, 0)
-        lowE(2, 0)
-        iE(3, 1)
-        lowQ(0)
-        lowE(2, 1)
-        lowQ(1)
-        lowQ(2)
-        lowE(3, 0)
-        sP()
-        sqT()
-        lowE(3, 1)
-        sqE()
-        lowQ(3)
-        iQ(0)
-        wP(1)
-        wP(0)
-        iQ(3)
-        S2(0, 0, 0)
-        E2(0, 0, 0)
-        S2(0, 0, 1)
-        E2(0, 0, 1)
-        S2(0, 1, 0)
-        E2(0, 1, 0)
-        S2(0, 1, 1)
-        E2(0, 1, 1)
-        S2(0, 2, 0)
-        E2(0, 2, 0)
-        S2(0, 2, 1)
-        E2(0, 2, 1)
-        S2(0, 3, 0)
-        E2(0, 3, 0)
-        S2(0, 3, 1)
-        E2(0, 3, 1)
-        S2(1, 0, 0)
-        E2(1, 0, 0)
-        S2(1, 0, 1)
-        E2(1, 0, 1)
-        S2(1, 1, 0)
-        E2(1, 1, 0)
-        fC(2)
-        S1(0, 0)
-        E1(0, 0)
-        iQ(1)
-        fQ(2)
-        fC(3)
-        S2(1, 1, 1)
-        E2(1, 1, 1)
-        S2(1, 2, 0)
-        E2(1, 2, 0)
-        S1(0, 1)
-        E1(0, 1)
-        Q2(0, 0)
-        Q2(0, 1)
-        S2(1, 2, 1)
-        E2(1, 2, 1)
-        S2(1, 3, 0)
-        E2(1, 3, 0)
-        S1(0, 2)
-        E1(0, 2)
-        Q2(1, 0)
-        Q1(0, 0)
-        S2(1, 3, 1)
-        E2(1, 3, 1)
-        S2(2, 0, 0)
-        E2(2, 0, 0)
-        S1(0, 3)
-        E1(0, 3)
-        fQ(3)
-        S2(2, 0, 1)
-        E2(2, 0, 1)
-        S2(2, 1, 0)
-        E2(2, 1, 0)
-        S2(2, 1, 1)
-        E2(2, 1, 1)
-        S1(1, 0)
-        E1(1, 0)
-        Q2(1, 1)
-        Q1(0, 1)
-        iQ(2)
-        S2(2, 2, 0)
-        E2(2, 2, 0)
-        S2(2, 2, 1)
-        E2(2, 2, 1)
-        S1(1, 1)
-        E1(1, 1)
-        Q2(2, 0)
-        S2(2, 3, 0)
-        E2(2, 3, 0)
-        S2(2, 3, 1)
-        E2(2, 3, 1)
-        S1(1, 2)
-        E1(1, 2)
-        Q1(1, 0)
-        S2(3, 0, 0)
-        E2(3, 0, 0)
-        S2(3, 0, 1)
-        E2(3, 0, 1)
-        S3(0, 0)
-        OV(0, 0)
-        S1(1, 3)
-        E1(1, 3)
-        Q2(2, 1)
-        ST(0, 0)
-        S2(3, 1, 0)
-        E2(3, 1, 0)
-        S2(3, 1, 1)
-        E2(3, 1, 1)
-        S2(3, 2, 0)
-        E2(3, 2, 0)
-        S3(0, 1)
-        OV(0, 1)
-        S1(2, 0)
-        E1(2, 0)
-        Q1(1, 1)
-        ST(0, 1)
-        S2(3, 2, 1)
-        E2(3, 2, 1)
-        S2(3, 3, 0)
-        E2(3, 3, 0)
-        S3(0, 2)
-        OV(0, 2)
-        S1(2, 1)
-        E1(2, 1)
-        Q2(3, 0)
-        ST(0, 2)
-        S2(3, 3, 1)
-        E2(3, 3, 1)
-        S1(2, 2)
-        E1(2, 2)
-        Q1(2, 0)
-        S3(1, 0)
-        OV(1, 0)
-        S1(2, 3)
-        E1(2, 3)
-        Q2(3, 1)
-        ST(1, 0)
-        S3(1, 1)
-        OV(1, 1)
-        S1(3, 0)
-        E1(3, 0)
-        Q1(2, 1)
-        ST(1, 1)
-        S3(1, 2)
-        OV(1, 2)
-        S1(3, 1)
-        E1(3, 1)
-        ST(1, 2)
-        S3(0, 3)
-        OV(0, 3)
-        S1(3, 2)
-        E1(3, 2)
-        Q1(3, 0)
-        ST(0, 3)
-        S3(1, 3)
-        OV(1, 3)
-        S1(3, 3)
-        E1(3, 3)
-        ST(1, 3)
-        S3(2, 0)
-        OV(2, 0)
-        Q1(3, 1)
-        ST(2, 0)
-        S3(2, 1)
-        OV(2, 1)
-        ST(2, 1)
-        S3(2, 2)
-        OV(2, 2)
-        ST(2, 2)
-        S3(2, 3)
-        OV(2, 3)
-        ST(2, 3)
-        S3(3, 0)
-        OV(3, 0)
-        ST(3, 0)
-        S3(3, 1)
-        OV(3, 1)
-        ST(3, 1)
-        S3(3, 2)
-        OV(3, 2)
-        ST(3, 2)
-        S3(3, 3)
-        OV(3, 3)
-        ST(3, 3)
+        for a in range(NA):
+            widen_initial(a)
+            transpose_initial(a)
+        interleave_final(0)
+        interleave_final(1)
+        for a in range(NA):
+            for g in range(KP):
+                scale_initial(a, g)
+        quantise_final(0)
+        for g in range(NG):
+            for half in range(2):
+                transpose_lowering(g, half)
+                group_lowering(g, half)
+            if g > 0:
+                quantise_lowering(g - 1)
+            if g == 1:
+                quantise_final(1)
+        move_words(0)
+        quantise_lowering(NG - 1)
+        quantise_initial(0)
+        spread_squeeze()
+        move_scales()
+        move_words(1)
+        quantise_initial(1)
+
+        put_off = {
+            0: [(quantise_final, (2,))],
+            2: [(interleave_final, (3,))],
+            3: [(quantise_final, (3,))],
+            5: [(quantise_initial, (2,))],
+            6: [(quantise_initial, (3,))],
+        }
+        owed = []
+        complete_left, complete_right = {}, {}
+        overlaps = []
+
+        def run_right(numbers, step):
+            for number in numbers:
+                right_unit(number)
+                f, g, half = units[number]
+                if half == 1 and g % 2 == 1:
+                    owed.append((step + 1, quantise_right, (f, g // 2)))
+                if half == 1 and g == NG - 1:
+                    complete_right[f] = step
+
+        def ready(pair):
+            return WAIT + max(complete_left[pair[0]], complete_right[pair[1]])
+
+        def open_pairs():
+            pairs = [(a, f) for a in complete_left for f in complete_right if (a, f) not in overlaps]
+            return sorted(pairs, key=ready)
+
+        run_right(range(LEAD), 0)
+        interleave_final(2)
+        done = LEAD
+        for step in range(NA * NG):
+            a, g = divmod(step, NG)
+            left_step(a, g)
+            if g == NG - 1:
+                complete_left[a] = step
+            for due, call, arguments in owed:
+                if due <= step:
+                    call(*arguments)
+            owed = [item for item in owed if item[0] > step]
+            for call, arguments in put_off.get(step, []):
+                call(*arguments)
+            if g % 2 == 1:
+                owed.append((step + 1, quantise_left, (a, g // 2)))
+            upto = min(len(units), LEAD + int(UNITS_PER_STEP * (step + 1)))
+            run_right(range(done, upto), step + 1)
+            done = upto
+            for pair in open_pairs()[:1]:
+                if ready(pair) <= step:
+                    overlaps.append(pair)
+                    make_overlap(*pair)
+                    owed.append((step + 1, make_strength, pair))
+        for due, call, arguments in owed:
+            call(*arguments)
+        for pair in open_pairs():
+            make_overlap(*pair)
+            make_strength(*pair)

from contextlib import ExitStack

import concourse.mybir as mybir
from concourse.masks import make_identity

I, B, G, C, F = 512, 1024, 2048, 512, 1024
FLOPS = 2 * I * B * G + 2 * G * C * F + 2 * I * G * F

F32 = mybir.dt.float32
BF16 = mybir.dt.bfloat16
I32 = mybir.dt.int32
U32 = mybir.dt.uint32
U8 = mybir.dt.uint8
FP8 = mybir.dt.float8_e4m3fn
FP8X4 = mybir.dt.float8_e4m3fn_x4
FP4X4 = mybir.dt.float4_e2m1fn_x4
MULT = mybir.AluOpType.mult

P = 128
T = 4
PASS = P * T
KP = B // PASS
NA = I // P
NG = G // PASS
NF = 4
FQ = F // NF
BANK = 512
RUN = 8

LEAD = 11
UNITS_PER_STEP = 2.25
WAIT = 3
RIGHT_ON_VECTOR = (LEAD - 1,)
WIDEN_ON_SCALAR = (3,)
INTERLEAVE_ON_VECTOR = (2, 3)
STORED_IN_HALVES = ((2, 0), (2, 1), (3, 0))


def tile_franck_condon_overlap_table_s11_kernel(
    tc, initial_bytes, initial_scale, raising_words, raising_scales, squeeze, lowering, final, population, out_0, out_1
):
    nc = tc.nc
    with ExitStack() as ctx:
        sbuf = ctx.enter_context(tc.tile_pool(name="sbuf", bufs=1))
        psum = ctx.enter_context(tc.psum_pool(name="psum", bufs=8))

        def keep(name, shape, dtype):
            kept = sbuf.tile(shape, dtype, name=name, tag=name, align_bytes=256)
            return kept

        def bank(dtype=F32):
            taken = psum.tile([P, BANK], dtype, name="bank", tag="bank")
            return taken

        def copy(on_vector, out, in_):
            if on_vector:
                nc.vector.tensor_copy(out=out, in_=in_)
            else:
                nc.scalar.copy(out=out, in_=in_)

        ctx.enter_context(tc.manual_schedule())

        bytes_in = keep("bytes_in", [P, NA, B], U8)
        k_scale = keep("k_scale", [P, KP, T], F32)
        low_rows = [keep("low_rows%d" % g, [P, T, C], BF16) for g in range(NG)]
        fin_rows = [keep("fin_rows%d" % h, [P, T, F // 2], BF16) for h in range(2)]
        words_in = [keep("words_in%d" % g, [P, 2 * G], U8) for g in range(KP)]
        scales_in = keep("scales_in", [P, KP, G], U8)
        squeeze_rows = keep("squeeze_rows", [P, P], BF16)
        pop = keep("pop", [P, NA], BF16)
        ident_f32 = keep("ident_f32", [P, P], F32)
        ident_bf16 = keep("ident_bf16", [P, P], BF16)
        by_slot = keep("by_slot", [P, P], F32)
        table_load = keep("table_load", [P, 1], F32)

        nc.vector.memset(scales_in[:].rearrange("p g n -> p (g n)").bitcast(I32), 0)
        nc.vector.memset(squeeze_rows[:], 0.0)
        nc.vector.memset(table_load[:], 0.0)
        nc.scalar.dma_start(out=k_scale[:], in_=initial_scale.rearrange("o (g p t) -> p (o g) t", p=P, t=T))
        nc.scalar.copy(out=table_load[:], in_=table_load[:])
        make_identity(nc, ident_f32[:])
        make_identity(nc, ident_bf16[:])

        states = initial_bytes.rearrange("(m a) k -> m a k", a=NA)
        low_groups = lowering.rearrange("(g m s) c -> g m s c", m=P, s=T)
        fin_passes = final.rearrange("(p t) f -> p t f", t=T)
        for h in range(2):
            nc.sync.dma_start(out=bytes_in[:, 2 * h : 2 * h + 2, :], in_=states[:, 2 * h : 2 * h + 2, :])
        nc.sync.dma_start(out=fin_rows[0][:], in_=fin_passes[:, :, : F // 2])
        for g in range(NG):
            nc.sync.dma_start(out=low_rows[g][:], in_=low_groups[g])
        nc.sync.dma_start(out=words_in[0][:].bitcast(I32), in_=raising_words[0].bitcast(I32))
        for quad in range(4):
            nc.sync.dma_start(
                out=scales_in[32 * quad : 32 * quad + 4, :, :].bitcast(I32),
                in_=raising_scales[:, 4 * quad : 4 * quad + 4, :].rearrange("g row n -> row g n").bitcast(I32),
            )
        nc.sync.dma_start(out=words_in[1][:].bitcast(I32), in_=raising_words[1].bitcast(I32))
        nc.sync.dma_start(out=fin_rows[1][:], in_=fin_passes[:, :, F // 2 :])
        for g in range(NG):
            nc.scalar.dma_start(
                out=squeeze_rows[T * g : T * g + T, :].rearrange("t (q r) -> t q r", r=RUN),
                in_=squeeze[PASS * g : PASS * (g + 1)].rearrange("(q t r) -> t q r", t=T, r=RUN),
            )
        nc.scalar.dma_start(out=pop[:], in_=population.rearrange("(m a) -> m a", a=NA))

        nc.vector.tensor_copy(
            out=by_slot[:].rearrange("p (t q h) -> p t q h", t=T, h=2),
            in_=ident_f32[:].rearrange("p (q t h) -> p t q h", t=T, h=2),
        )

        ini_bf16 = keep("ini_bf16", [P, NA, B], BF16)
        ini_grouped = [keep("ini_grouped%d" % a, [P, KP * P * T], BF16) for a in range(NA)]
        ini_codes = [keep("ini_codes%d" % a, [P, KP * P], U32) for a in range(NA)]
        ini_scales = [keep("ini_scales%d" % a, [P, KP * P], U8) for a in range(NA)]
        low_grouped = [keep("low_grouped%d" % g, [P, PASS * T], BF16) for g in range(NG)]
        low_codes = [keep("low_codes%d" % g, [P, PASS], U32) for g in range(NG)]
        low_scales = [keep("low_scales%d" % g, [P, PASS], U8) for g in range(NG)]
        fin_grouped = [keep("fin_grouped%d" % f, [P, FQ * T], BF16) for f in range(NF)]
        fin_codes = [keep("fin_codes%d" % f, [P, FQ], U32) for f in range(NF)]
        fin_scales = [keep("fin_scales%d" % f, [P, FQ], U8) for f in range(NF)]
        words = [keep("words%d" % g, [P, 2 * G], U8) for g in range(KP)]
        scales = keep("scales", [P, KP, G], U8)
        squeeze_by_slot = keep("squeeze_by_slot", [P, NG * T], F32)
        left_grouped = [keep("left_grouped%d" % a, [P, NG * P * T], BF16) for a in range(NA)]
        left_codes = [keep("left_codes%d" % a, [P, NG * P], U32) for a in range(NA)]
        left_scales = [keep("left_scales%d" % a, [P, NG * P], U8) for a in range(NA)]
        right_grouped = [
            sbuf.tile([P, NG * FQ * T], BF16, name="right_grouped%d" % f, tag="right_grouped", bufs=2, align_bytes=256)
            for f in range(NF)
        ]
        right_codes = [keep("right_codes%d" % f, [P, NG * FQ], U32) for f in range(NF)]
        right_scales = [keep("right_scales%d" % f, [P, NG * FQ], U8) for f in range(NF)]
        overlap = keep("overlap", [P, NA, F], F32)
        strength = keep("strength", [P, NA, F], F32)

        ini_banks = {}

        def widen_initial(a):
            copy(a not in WIDEN_ON_SCALAR, ini_bf16[:, a, :], bytes_in[:, a, :].bitcast(FP8))

        def transpose_initial(a):
            pairs = ini_bf16[:, a, :].bitcast(F32)
            ini_banks[a] = bank()
            for g in range(KP):
                for u in range(2):
                    at = (2 * g + u) * P
                    every_second = slice(PASS // 2 * g + u, PASS // 2 * (g + 1), 2)
                    nc.tensor.transpose(ini_banks[a][:, at : at + P], pairs[:, every_second], ident_f32[:])

        def scale_initial(a, g):
            pairs = ini_banks[a][:, 2 * P * g : 2 * P * (g + 1)].bitcast(BF16)
            nc.vector.tensor_tensor(
                out=ini_grouped[a][:, P * T * g : P * T * (g + 1)].rearrange("p (m u e) -> p m u e", u=2, e=2),
                in0=pairs.rearrange("p (u m e) -> p m u e", u=2, e=2),
                in1=k_scale[:, g, :].rearrange("p (u e) -> p u e", u=2).unsqueeze(1).to_broadcast([P, P, 2, 2]),
                op=MULT,
            )

        def quantise_initial(a):
            nc.vector.quantize_mx(out=ini_codes[a][:].bitcast(FP8X4), scales=ini_scales[a][:], in_=ini_grouped[a][:])

        def interleave_final(f):
            cols = slice(FQ * (f % 2), FQ * (f % 2 + 1))
            copy(
                f in INTERLEAVE_ON_VECTOR,
                fin_grouped[f][:].rearrange("p (n i t) -> p n t i", i=4, t=T),
                fin_rows[f // 2][:, :, cols].rearrange("p t (n i) -> p n t i", i=4),
            )

        def quantise_final(f):
            nc.vector.quantize_mx(out=fin_codes[f][:].bitcast(FP8X4), scales=fin_scales[f][:], in_=fin_grouped[f][:])

        low_banks = {}

        def transpose_lowering(g, half):
            pairs = low_rows[g][:].rearrange("m s c -> m (s c)").bitcast(F32)
            low_banks[(g, half)] = bank()
            for x in range(4):
                s, u = 2 * half + x // 2, x % 2
                every_second = slice(C // 2 * s + u, C // 2 * (s + 1), 2)
                nc.tensor.transpose(low_banks[(g, half)][:, x * P : (x + 1) * P], pairs[:, every_second], by_slot[:])

        def group_lowering(g, half):
            by_column = low_grouped[g][:].bitcast(F32).rearrange("p (j x) -> p j x", x=8)
            copy(False, by_column[:, :, 4 * half : 4 * half + 4], low_banks[(g, half)][:].rearrange("p (x j) -> p j x", x=4))

        def quantise_lowering(g):
            nc.vector.quantize_mx(out=low_codes[g][:].bitcast(FP8X4), scales=low_scales[g][:], in_=low_grouped[g][:])

        def move_words(g):
            nc.vector.tensor_copy(
                out=words[g][:].bitcast(I32).rearrange("p (n t q w) -> p n t q w", n=NG, t=T, w=RUN // 2),
                in_=words_in[g][:].bitcast(I32).rearrange("p (n q t w) -> p n t q w", n=NG, t=T, w=RUN // 2),
            )

        def move_scales():
            for g in range(KP):
                nc.vector.tensor_copy(
                    out=scales[:, g, :].bitcast(I32).rearrange("p (n t q w) -> p n t q w", n=NG, t=T, w=RUN // 4),
                    in_=scales_in[:, g, :].bitcast(I32).rearrange("p (n q t w) -> p n t q w", n=NG, t=T, w=RUN // 4),
                )

        def spread_squeeze():
            turned = bank(BF16)
            nc.tensor.transpose(turned[:, :P], squeeze_rows[:], ident_bf16[:])
            nc.vector.tensor_copy(out=squeeze_by_slot[:], in_=turned[:, : NG * T])

        def left_step(a, g):
            sums = bank()
            for t in range(T):
                slot = slice(P * (T * g + t), P * (T * g + t + 1))
                for k in range(KP):
                    nc.tensor.matmul_mx(
                        out=sums[:, P * t : P * (t + 1)],
                        lhsT=words[k][:, 2 * slot.start : 2 * slot.stop].bitcast(FP4X4),
                        lhsT_scale=scales[:, k, slot],
                        rhs=ini_codes[a][:, P * k : P * (k + 1)].bitcast(FP8X4),
                        rhs_scale=ini_scales[a][:, P * k : P * (k + 1)],
                        start=(k == 0),
                        stop=(k == KP - 1),
                    )
            nc.vector.tensor_tensor(
                out=left_grouped[a][:, P * T * g : P * T * (g + 1)].rearrange("p (m t) -> p m t", t=T),
                in0=sums[:].rearrange("p (t m) -> p m t", t=T),
                in1=squeeze_by_slot[:, T * g : T * (g + 1)].unsqueeze(1).to_broadcast([P, P, T]),
                op=MULT,
            )

        def quantise_left(a, pair):
            cols = slice(2 * P * pair, 2 * P * (pair + 1))
            nc.vector.quantize_mx(
                out=left_codes[a][:, cols].bitcast(FP8X4),
                scales=left_scales[a][:, cols],
                in_=left_grouped[a][:, T * cols.start : T * cols.stop],
            )

        units = [(f, g, half) for f in range(NF) for g in range(NG) for half in range(2)]

        def right_unit(number):
            f, g, half = units[number]
            cols = slice(P * half, P * (half + 1))
            sums = bank()
            for t in range(T):
                slot = slice(P * t, P * (t + 1))
                nc.tensor.matmul_mx(
                    out=sums[:, slot],
                    lhsT=low_codes[g][:, slot].bitcast(FP8X4),
                    lhsT_scale=low_scales[g][:, slot],
                    rhs=fin_codes[f][:, cols].bitcast(FP8X4),
                    rhs_scale=fin_scales[f][:, cols],
                    start=True,
                    stop=True,
                )
            at = T * (FQ * g + P * half)
            copy(
                number in RIGHT_ON_VECTOR,
                right_grouped[f][:, at : at + T * P].rearrange("p (n t) -> p n t", t=T),
                sums[:].rearrange("p (t n) -> p n t", t=T),
            )

        def quantise_right(f, pair):
            cols = slice(2 * FQ * pair, 2 * FQ * (pair + 1))
            nc.vector.quantize_mx(
                out=right_codes[f][:, cols].bitcast(FP8X4),
                scales=right_scales[f][:, cols],
                in_=right_grouped[f][:, T * cols.start : T * cols.stop],
            )

        overlap_banks = {}

        def store(out, made, a, f):
            if (a, f // 2) not in STORED_IN_HALVES:
                cols = slice(FQ * f, FQ * (f + 1))
            elif f % 2 == 1:
                cols = slice(FQ * (f - 1), FQ * (f + 1))
            else:
                return
            nc.sync.dma_start(out=out.rearrange("(m a) f -> m a f", a=NA)[:, a, cols], in_=made[:, a, cols])

        def make_overlap(a, f):
            sums = bank()
            overlap_banks[(a, f)] = sums
            for g in range(NG):
                nc.tensor.matmul_mx(
                    out=sums[:, :FQ],
                    lhsT=left_codes[a][:, P * g : P * (g + 1)].bitcast(FP8X4),
                    lhsT_scale=left_scales[a][:, P * g : P * (g + 1)],
                    rhs=right_codes[f][:, FQ * g : FQ * (g + 1)].bitcast(FP8X4),
                    rhs_scale=right_scales[f][:, FQ * g : FQ * (g + 1)],
                    start=(g == 0),
                    stop=(g == NG - 1),
                )
            nc.scalar.copy(out=overlap[:, a, FQ * f : FQ * (f + 1)], in_=sums[:, :FQ])
            store(out_0, overlap, a, f)

        def make_strength(a, f):
            cols = slice(FQ * f, FQ * (f + 1))
            nc.vector.scalar_tensor_tensor(
                out=strength[:, a, cols],
                in0=overlap_banks[(a, f)][:, :FQ],
                scalar=pop[:, a : a + 1],
                in1=overlap[:, a, cols],
                op0=MULT,
                op1=MULT,
            )
            store(out_1, strength, a, f)

        for a in range(NA):
            widen_initial(a)
            transpose_initial(a)
        interleave_final(0)
        interleave_final(1)
        for a in range(NA):
            for g in range(KP):
                scale_initial(a, g)
        quantise_final(0)
        for g in range(NG):
            for half in range(2):
                transpose_lowering(g, half)
                group_lowering(g, half)
            if g > 0:
                quantise_lowering(g - 1)
            if g == 1:
                quantise_final(1)
        move_words(0)
        quantise_lowering(NG - 1)
        quantise_initial(0)
        spread_squeeze()
        move_scales()
        move_words(1)
        quantise_initial(1)

        put_off = {
            0: [(quantise_final, (2,))],
            2: [(interleave_final, (3,))],
            3: [(quantise_final, (3,))],
            5: [(quantise_initial, (2,))],
            6: [(quantise_initial, (3,))],
        }
        owed = []
        complete_left, complete_right = {}, {}
        overlaps = []

        def run_right(numbers, step):
            for number in numbers:
                right_unit(number)
                f, g, half = units[number]
                if half == 1 and g % 2 == 1:
                    owed.append((step + 1, quantise_right, (f, g // 2)))
                if half == 1 and g == NG - 1:
                    complete_right[f] = step

        def ready(pair):
            return WAIT + max(complete_left[pair[0]], complete_right[pair[1]])

        def open_pairs():
            pairs = [(a, f) for a in complete_left for f in complete_right if (a, f) not in overlaps]
            return sorted(pairs, key=ready)

        run_right(range(LEAD), 0)
        interleave_final(2)
        done = LEAD
        for step in range(NA * NG):
            a, g = divmod(step, NG)
            left_step(a, g)
            if g == NG - 1:
                complete_left[a] = step
            for due, call, arguments in owed:
                if due <= step:
                    call(*arguments)
            owed = [item for item in owed if item[0] > step]
            for call, arguments in put_off.get(step, []):
                call(*arguments)
            if g % 2 == 1:
                owed.append((step + 1, quantise_left, (a, g // 2)))
            upto = min(len(units), LEAD + int(UNITS_PER_STEP * (step + 1)))
            run_right(range(done, upto), step + 1)
            done = upto
            for pair in open_pairs()[:1]:
                if ready(pair) <= step:
                    overlaps.append(pair)
                    make_overlap(*pair)
                    owed.append((step + 1, make_strength, pair))
        for due, call, arguments in owed:
            call(*arguments)
        for pair in open_pairs():
            make_overlap(*pair)
            make_strength(*pair)
